import numpy as np
import ml_dtypes


def mxq(x, axis, fmt="e4m3"):
    dtype, down = {"e4m3": (ml_dtypes.float8_e4m3fn, 7), "e5m2": (ml_dtypes.float8_e5m2, 14)}[fmt]
    v = np.moveaxis(np.asarray(x, np.float32).astype(ml_dtypes.bfloat16).astype(np.float64), axis, -1)
    blocks = v.reshape(v.shape[:-1] + (-1, 32))
    amax = np.abs(blocks).max(-1, keepdims=True)
    byte = np.maximum(np.where(amax > 0, np.frexp(amax)[1] - 1 + 127, 0) - down, 1)
    scale = np.exp2(byte - 127.0)
    codes = (blocks / scale).astype(np.float32).astype(dtype).astype(np.float64)
    return np.moveaxis((codes * scale).reshape(v.shape), -1, axis)


WIDE = False


def mx_kscale(k):
    if not WIDE:
        return np.ones(k)
    levels = np.array([10, -10, 5, -5, 0])
    if k % 512:
        return np.exp2(np.random.permutation(np.resize(levels, k // 32))).repeat(32)
    a = np.empty((k // 512, 16))
    for p in range(k // 512):
        a[p, :8] = np.random.permutation(np.resize(levels, 8))
        for g in range(8):
            far = levels[np.abs(levels - a[p, g]) >= 10]
            a[p, g + 8] = far[np.random.randint(len(far))]
    return np.exp2(a.ravel()).repeat(32)


BF16 = ml_dtypes.bfloat16


def bf(x):
    return np.asarray(x, np.float32).astype(BF16)


def f64(x):
    return np.asarray(x).astype(np.float64)


E2M1 = np.array([0.0, 0.5, 1.0, 1.5, 2.0, 3.0, 4.0, 6.0, -0.0, -0.5, -1.0, -1.5, -2.0, -3.0, -4.0, -6.0])


def pack_weight(w, fmt):
    k, n = w.shape
    w = f64(bf(w)).reshape(k // 32, 32, n)
    amax = np.abs(w).max(1)
    if fmt == "e4m3":
        byte = np.frexp(amax)[1] - 1 + 127 - 7
    else:
        mant, ex = np.frexp(amax / 6.0)
        byte = np.where(mant > 0.5, ex, ex - 1) + 127
    byte = np.clip(np.where(amax > 0, byte, 1), 1, 254)
    scaled = (w * np.exp2(127.0 - byte)[:, None, :]).reshape(k, n).astype(np.float32)
    by_word = np.ascontiguousarray(scaled.reshape(k // 512, 128, 4, n).transpose(0, 1, 3, 2))
    if fmt == "e4m3":
        words = by_word.astype(ml_dtypes.float8_e4m3fn).view(np.uint8)
    else:
        c = by_word.astype(ml_dtypes.float4_e2m1fn).view(np.uint8) & 0xF
        words = c[..., 0::2] | (c[..., 1::2] << 4)
    return np.ascontiguousarray(words), np.ascontiguousarray(byte.astype(np.uint8).reshape(k // 512, 16, n))


def unpack_weight(words, scales, fmt):
    g, p, n, _ = words.shape
    if fmt == "e4m3":
        vals = np.ascontiguousarray(words).view(ml_dtypes.float8_e4m3fn).astype(np.float64)
    else:
        nib = np.empty((g, p, n, 4), np.uint8)
        nib[..., 0::2] = words & 0xF
        nib[..., 1::2] = words >> 4
        vals = E2M1[nib]
    vals = vals * np.repeat(np.exp2(scales.astype(np.float64) - 127.0), 8, axis=1)[..., None]
    return vals.transpose(0, 1, 3, 2).reshape(g * 512, n)
def pack4(w):
    words, scales = pack_weight(w, "e2m1")
    return words.reshape(words.shape[0], 128, -1), scales


def unpack4(words, scales):
    return unpack_weight(words.reshape(words.shape[0], 128, -1, 2), scales, "e2m1")


def planes(Y):
    n, m = Y.shape
    b = f64(bf(Y)).reshape(n // 32, 32, m)
    amax = np.abs(b).max(1)
    byte = np.clip(np.where(amax > 0, np.frexp(amax)[1] - 1 + 127 - 7, 1), 1, 254)
    codes = (b * np.exp2(127.0 - byte)[:, None, :]).reshape(n, m).astype(np.float32).astype(ml_dtypes.float8_e4m3fn).view(np.uint8)
    words = codes.reshape(n // 512, 128, 4, m).transpose(0, 1, 3, 2)
    return np.ascontiguousarray(words), np.ascontiguousarray(byte.astype(np.uint8).reshape(n // 512, 16, m))


B, S, D, M, N, C = 2, 1024, 512, 512, 512, 2


def cauchy_parts(om, nu, b):
    de = om[:, None] - nu[None, :]
    w = b[None, :] / (0.25 + de * de)
    gr = 0.5 * w
    gi = -de * w
    return gr, gi


def setup_inputs():
    s, t, r = mx_kscale(S), mx_kscale(M), mx_kscale(N)
    x = bf(np.random.standard_normal((B, S, D)) / s[None, :, None])
    p = np.random.standard_normal((M, S)) / np.sqrt(S) * s[None, :] * t[:, None]
    p_words, p_scales = pack4(p.T)
    om = bf(np.random.uniform(-4.0, 4.0, M))
    nu = bf(np.random.uniform(-4.0, 4.0, N))
    b = bf(np.random.standard_normal(N) * r)
    c = np.random.standard_normal((N, D)) * 1.5 / np.sqrt(N) / r[:, None]
    c_words, c_scales = pack4(c)
    q = bf(np.random.standard_normal((C, S, M)) / np.sqrt(M) / t[None, None, :])
    return {"x": x,
            "p_words": p_words,
            "p_scales": p_scales,
            "om": om,
            "nu": nu,
            "b": b,
            "c_words": c_words,
            "c_scales": c_scales,
            "q": q}


def core(x, p_words, p_scales, om, nu, b, c_words, c_scales, q):
    gr, gi = cauchy_parts(f64(om), f64(nu), f64(b))
    gr, gi = gr, gi
    cq = unpack4(c_words, c_scales)
    kr = mxq(gr, 1, "e4m3") @ cq
    ki = mxq(gi, 1, "e4m3") @ cq
    u = unpack4(p_words, p_scales).T @ mxq(f64(x), 1, "e4m3")
    fr = kr[None, :, :] * u
    fi = ki[None, :, :] * u
    qq = mxq(f64(q), 2, "e4m3")
    return (qq[0] @ mxq(fr, 1, "e4m3")) - (qq[1] @ mxq(fi, 1, "e4m3"))


def reference(x, p_words, p_scales, om, nu, b, c_words, c_scales, q):
    R_out = core(x, p_words, p_scales, om, nu, b, c_words, c_scales, q)
    words, scales = planes(np.moveaxis(R_out, 2, 0).reshape(512, -1))
    return R_out, words, scales

@@ -1,0 +1,485 @@
+from contextlib import ExitStack
+
+import concourse.mybir as mybir
+from concourse.masks import make_identity
+
+B, S, D, M, N = 2, 1024, 512, 512, 512
+FLOPS = 2 * (2 * M * N * D + B * M * S * D + 2 * B * S * M * D)
+
+F32 = mybir.dt.float32
+BF16 = mybir.dt.bfloat16
+I32 = mybir.dt.int32
+U32 = mybir.dt.uint32
+U8 = mybir.dt.uint8
+FP8X4 = mybir.dt.float8_e4m3fn_x4
+FP4X4 = mybir.dt.float4_e2m1fn_x4
+ALU = mybir.AluOpType
+ACT = mybir.ActivationFunctionType
+
+P = 128
+PACK = 4
+W = 512
+
+
+def tile_cauchytransferfunctionfilter_x2_kernel(
+    tc, x, p_words, p_scales, om, nu, b, c_words, c_scales, q, out_0, out_1, out_2
+):
+    nc = tc.nc
+    with ExitStack() as ctx:
+        sb = ctx.enter_context(tc.tile_pool(name="sb", bufs=1))
+        ps = ctx.enter_context(tc.psum_pool(name="ps", bufs=1))
+        ctx.enter_context(tc.manual_schedule())
+
+        def tile(name, shape, dtype):
+            return sb.tile(shape, dtype, name=name, align_bytes=64)
+
+        def tiles(name, count, shape, dtype):
+            return [tile("%s%d" % (name, i), shape, dtype) for i in range(count)]
+
+        bank = [ps.tile([P, W], F32, name="bank%d" % i) for i in range(8)]
+
+        ident_bf = tile("ident_bf", [P, P], BF16)
+        ident_f32 = tile("ident_f32", [P, P], F32)
+        warm_in = tile("warm_in", [P, 1], F32)
+        warm_out = tile("warm_out", [P, 1], F32)
+        om_col = tile("om_col", [P, PACK], BF16)
+        nu_col = tile("nu_col", [P, PACK], BF16)
+        b_col = tile("b_col", [P, PACK], BF16)
+        om_row = tile("om_row", [P, M], BF16)
+        dist = tile("dist", [P, PACK, M], F32)
+        lorentz = tile("lorentz", [P, M, PACK], F32)
+        de_b = tile("de_b", [P, PACK, M], F32)
+        g_bf = tiles("g_bf", 2, [P, M, PACK], BF16)
+        g_codes = tiles("g_codes", 2, [P, M], U32)
+        g_scale = tiles("g_scale", 2, [P, M], U8)
+        pw_raw = tile("pw_raw", [P, 2, 2 * M], U8)
+        psc_raw = tile("psc_raw", [P, 2, M], U8)
+        pw = tile("pw", [P, PACK, 2, 2 * P], U8)
+        psc = tile("psc", [P, PACK, 2, P], U8)
+        cw = tile("cw", [P, 2 * D], U8)
+        csc = tile("csc", [P, D], U8)
+        x_raw = tiles("x_raw", 4, [P, PACK, D], BF16)
+        x_bf = tiles("x_bf", 2, [P, D, PACK], BF16)
+        x_codes = tiles("x_codes", 4, [P, D], U32)
+        x_scale = tiles("x_scale", 4, [P, D], U8)
+        q_raw = tiles("q_raw", 4, [P, 2, 2 * M], BF16)
+        q_bf = tiles("q_bf", 4, [P, 2, 4 * 2 * P], BF16)
+        q_codes = tiles("q_codes", 4, [P, W], U32)
+        q_scale = tiles("q_scale", 4, [P, W], U8)
+        k_sb = tiles("k_sb", 2, [P, 4, W], F32)
+        f_bf = tiles("f_bf", 2, [P, D, PACK], BF16)
+        f_codes = tiles("f_codes", 4, [P, D], U32)
+        f_scale = tiles("f_scale", 4, [P, D], U8)
+        y32 = tiles("y32", 8, [P, 2, D], F32)
+        y_bf = tiles("y_bf", 3, [P, 2 * D], BF16)
+        yt_bf = tiles("yt_bf", 3, [P, 2 * D], BF16)
+        y_codes = tile("y_codes", [P, B * S], U32)
+        y_scale = tile("y_scale", [P, B * S], U8)
+
+        def load_col(dst, vec):
+            nc.sync.dma_start(out=dst[:], in_=vec.rearrange("(p t) -> p t", t=PACK))
+
+        def load_x(i):
+            bi, g = divmod(i, 2)
+            nc.sync.dma_start(
+                out=x_raw[i][:], in_=x[bi, W * g : W * (g + 1), :].rearrange("(p j) d -> p j d", j=PACK)
+            )
+
+        def load_q(i):
+            half, ci = divmod(i, 2)
+            nc.sync.dma_start(
+                out=q_raw[i][:],
+                in_=q[ci, W * half : W * (half + 1), :].rearrange("(a p h) m -> p a (h m)", a=2, h=2),
+            )
+
+        def load_p_words():
+            nc.sync.dma_start(out=pw_raw[:].bitcast(I32), in_=p_words.rearrange("g p n -> p g n").bitcast(I32))
+
+        def load_p_scales():
+            for quad in range(4):
+                nc.sync.dma_start(
+                    out=psc_raw[32 * quad : 32 * quad + 4, :, :].bitcast(I32),
+                    in_=p_scales[:, 4 * quad : 4 * quad + 4, :].rearrange("g r n -> r g n").bitcast(I32),
+                )
+
+        def load_c():
+            nc.sync.dma_start(out=cw[:].bitcast(I32), in_=c_words[0].bitcast(I32))
+            for quad in range(4):
+                nc.sync.dma_start(
+                    out=csc[32 * quad : 32 * quad + 4, :].bitcast(I32),
+                    in_=c_scales[0, 4 * quad : 4 * quad + 4, :].bitcast(I32),
+                )
+
+        def quantize(codes, scale, src):
+            nc.vector.quantize_mx(out=codes.bitcast(FP8X4), scales=scale, in_=src)
+
+        def flat(t):
+            return t[:].rearrange("p a b -> p (a b)")
+
+        def permute_p_words():
+            nc.vector.tensor_copy(
+                out=pw[:].rearrange("p t g (m e) -> p t (g m) e", e=2),
+                in_=pw_raw[:].rearrange("p g (m t e) -> p t (g m) e", t=PACK, e=2),
+            )
+
+        def permute_p_scales():
+            nc.vector.tensor_copy(
+                out=psc[:].rearrange("p t g m -> p t (g m)"),
+                in_=psc_raw[:].rearrange("p g (m t) -> p t (g m)", t=PACK),
+            )
+
+        def x_interleave(i, on_scalar=False):
+            dst = x_bf[i % 2][:].rearrange("p (c i) t -> p c t i", i=4)
+            src = x_raw[i][:].rearrange("p t (c i) -> p c t i", i=4)
+            if on_scalar:
+                nc.scalar.copy(out=dst, in_=src)
+            else:
+                nc.vector.tensor_copy(out=dst, in_=src)
+
+        def x_quantize(i):
+            quantize(x_codes[i][:], x_scale[i][:], flat(x_bf[i % 2]))
+
+        def spread_om():
+            view = bank[0][:].bitcast(BF16)
+            for t in range(PACK):
+                nc.tensor.transpose(
+                    view[:, P * t : P * (t + 1)], om_col[:, t : t + 1].to_broadcast([P, P]), ident_bf[:]
+                )
+            nc.scalar.copy(out=om_row[:], in_=view[:, 0:M])
+
+        def cols(half):
+            return slice(256 * half, 256 * (half + 1))
+
+        def lorentz_all():
+            for half in range(2):
+                for t in range(PACK):
+                    nc.scalar.activation(
+                        out=dist[:, t, cols(half)], in_=om_row[:, cols(half)], func=ACT.Square,
+                        bias=nu_col[:, t : t + 1], scale=-1.0,
+                    )
+            for half in range(2):
+                nc.scalar.activation(
+                    out=dist[:, :, cols(half)], in_=dist[:, :, cols(half)], func=ACT.Abs_reciprocal_sqrt, bias=0.25
+                )
+            for half in range(2):
+                nc.scalar.activation(
+                    out=lorentz[:, cols(half), :], in_=dist[:, :, cols(half)].rearrange("p t m -> p m t"),
+                    func=ACT.Square,
+                )
+
+        def de_times_b():
+            for t in range(PACK):
+                nc.vector.tensor_scalar(
+                    out=de_b[:, t, :], in0=om_row[:], scalar1=nu_col[:, t : t + 1], scalar2=b_col[:, t : t + 1],
+                    op0=ALU.subtract, op1=ALU.mult,
+                )
+
+        def g_real(half):
+            nc.vector.scalar_tensor_tensor(
+                out=g_bf[0][:, cols(half), :], in0=lorentz[:, cols(half), :], scalar=0.5,
+                in1=b_col[:].unsqueeze(1).to_broadcast([P, 256, PACK]), op0=ALU.mult, op1=ALU.mult,
+            )
+
+        def g_imag(half):
+            nc.vector.tensor_tensor(
+                out=g_bf[1][:, cols(half), :], in0=lorentz[:, cols(half), :],
+                in1=de_b[:, :, cols(half)].rearrange("p t m -> p m t"), op=ALU.mult,
+            )
+
+        def g_quantize(part):
+            quantize(g_codes[part][:], g_scale[part][:], flat(g_bf[part]))
+
+        def q_transpose(i, a, bk):
+            words = q_raw[i][:, a, :].bitcast(F32)
+            for h in range(2):
+                for u in range(2):
+                    nc.tensor.transpose(
+                        bank[bk][:, P * (2 * h + u) : P * (2 * h + u + 1)],
+                        words[:, 256 * h + u : 256 * (h + 1) : 2], ident_f32[:],
+                    )
+
+        def q_evict(i, a, bk):
+            nc.scalar.copy(
+                out=q_bf[i][:, a, :].bitcast(F32).rearrange("p (s r) -> p s r", r=4),
+                in_=bank[bk][:].rearrange("p (r s) -> p s r", r=4),
+            )
+
+        def q_quantize(i):
+            quantize(q_codes[i][:], q_scale[i][:], flat(q_bf[i]))
+
+        def u_matmul(bi, j, bk):
+            for t in range(PACK):
+                for g in range(2):
+                    nc.tensor.matmul_mx(
+                        out=bank[bk][:, P * t : P * (t + 1)],
+                        lhsT=pw[:, t, g, :].bitcast(FP4X4), lhsT_scale=psc[:, t, g, :],
+                        rhs=x_codes[2 * bi + g][:, P * j : P * (j + 1)].bitcast(FP8X4),
+                        rhs_scale=x_scale[2 * bi + g][:, P * j : P * (j + 1)],
+                        start=(g == 0), stop=(g == 1),
+                    )
+
+        def k_matmul(part, j, bk):
+            for t in range(PACK):
+                nc.tensor.matmul_mx(
+                    out=bank[bk][:, P * t : P * (t + 1)],
+                    lhsT=g_codes[part][:, P * t : P * (t + 1)].bitcast(FP8X4),
+                    lhsT_scale=g_scale[part][:, P * t : P * (t + 1)],
+                    rhs=cw[:, 2 * P * j : 2 * P * (j + 1)].bitcast(FP4X4),
+                    rhs_scale=csc[:, P * j : P * (j + 1)],
+                    start=True, stop=True,
+                )
+
+        def by_slot(bk):
+            return bank[bk][:].rearrange("p (t a e) -> p e a t", t=4, e=4)
+
+        def k_evict(part, j, bk):
+            nc.scalar.copy(out=k_sb[part][:, j, :].rearrange("p (e a t) -> p e a t", e=4, t=4), in_=by_slot(bk))
+
+        def f_product(part, j, bk):
+            nc.vector.tensor_tensor(
+                out=f_bf[part][:].rearrange("p (e w) t -> p e w t", e=4)[:, :, 32 * j : 32 * (j + 1), :],
+                in0=by_slot(bk),
+                in1=k_sb[part][:, j, :].rearrange("p (e a t) -> p e a t", e=4, t=4), op=ALU.mult,
+            )
+
+        def f_quantize(bi, part):
+            quantize(f_codes[2 * bi + part][:], f_scale[2 * bi + part][:], flat(f_bf[part]))
+
+        def y_matmul(pair, h, bk):
+            bi, blk = divmod(pair, 4)
+            half, a = divmod(blk, 2)
+            sl = slice(256 * a + P * h, 256 * a + P * (h + 1))
+            for part in range(2):
+                nc.tensor.matmul_mx(
+                    out=bank[bk][:],
+                    lhsT=q_codes[2 * half + part][:, sl].bitcast(FP8X4), lhsT_scale=q_scale[2 * half + part][:, sl],
+                    rhs=f_codes[2 * bi + part][:].bitcast(FP8X4), rhs_scale=f_scale[2 * bi + part][:],
+                    start=(part == 0), stop=(part == 1),
+                )
+
+        def copy_on(on_vector, dst, src):
+            if on_vector:
+                nc.vector.tensor_copy(out=dst, in_=src)
+            else:
+                nc.scalar.copy(out=dst, in_=src)
+
+        def y_evict(pair, h, bk, on_vector=False):
+            copy_on(
+                on_vector,
+                y32[pair][:, h, :].rearrange("p (w e) -> p w e", e=4),
+                bank[bk][:].rearrange("p (e w) -> p w e", e=4),
+            )
+
+        def yt_matmul(pair, h, bk):
+            bi, blk = divmod(pair, 4)
+            half, a = divmod(blk, 2)
+            sl = slice(256 * a + P * h, 256 * a + P * (h + 1))
+            for t in range(PACK):
+                ch = slice(P * t, P * (t + 1))
+                for part in range(2):
+                    nc.tensor.matmul_mx(
+                        out=bank[bk][:, ch],
+                        lhsT=f_codes[2 * bi + part][:, ch].bitcast(FP8X4), lhsT_scale=f_scale[2 * bi + part][:, ch],
+                        rhs=q_codes[2 * half + part][:, sl].bitcast(FP8X4), rhs_scale=q_scale[2 * half + part][:, sl],
+                        start=(part == 0), stop=(part == 1),
+                    )
+
+        def yt_round(pair, h, bk, on_vector=False):
+            copy_on(
+                on_vector,
+                yt_bf[pair % 3][:, W * h : W * (h + 1)].rearrange("p (s t) -> p s t", t=4),
+                bank[bk][:].rearrange("p (t s) -> p s t", t=4),
+            )
+
+        def y_store_h(pair, h):
+            bi, blk = divmod(pair, 4)
+            lo = 256 * blk + P * h
+            nc.sync.dma_start(out=out_0[bi, lo : lo + P, :], in_=y32[pair][:, h, :])
+
+        def y_store(pair):
+            bi, blk = divmod(pair, 4)
+            nc.sync.dma_start(
+                out=out_0[bi, 256 * blk : 256 * (blk + 1), :].rearrange("(h p) d -> p h d", h=2),
+                in_=y32[pair][:],
+            )
+
+        def y_round(pair):
+            nc.vector.tensor_copy(
+                out=y_bf[pair % 3][:].rearrange("p (u w e) -> p u w e", u=2, e=2),
+                in_=flat(y32[pair]).rearrange("p (w u e) -> p u w e", u=2, e=2),
+            )
+
+        def y_transpose(pair, bk):
+            words = y_bf[pair % 3][:].bitcast(F32)
+            for r in range(4):
+                nc.tensor.transpose(bank[bk][:, P * r : P * (r + 1)], words[:, P * r : P * (r + 1)], ident_f32[:])
+
+        def yt_evict(pair, bk, on_vector=False):
+            copy_on(
+                on_vector,
+                yt_bf[pair % 3][:].bitcast(F32).rearrange("p (w u) -> p w u", u=2),
+                bank[bk][:].rearrange("p (u w) -> p w u", u=2),
+            )
+
+        def y_quantize(pair):
+            sl = slice(256 * pair, 256 * (pair + 1))
+            quantize(y_codes[:, sl], y_scale[:, sl], yt_bf[pair % 3][:])
+
+        def words_store(lo, hi):
+            sl = slice(256 * lo, 256 * hi)
+            nc.sync.dma_start(
+                out=out_1[0].rearrange("p m t -> p (m t)").bitcast(I32)[:, sl], in_=y_codes[:, sl].bitcast(I32)
+            )
+
+        def scales_store(lo, hi):
+            sl = slice(256 * lo, 256 * hi)
+            for quad in range(4):
+                nc.sync.dma_start(
+                    out=out_2[0, 4 * quad : 4 * quad + 4, sl].bitcast(I32),
+                    in_=y_scale[32 * quad : 32 * quad + 4, sl].bitcast(I32),
+                )
+
+        def setup():
+            nc.vector.memset(warm_in[:], 1.0)
+            nc.vector.memset(flat(psc_raw).bitcast(I32), 0)
+            nc.vector.memset(csc[:].bitcast(I32), 0)
+            nc.scalar.activation(out=warm_out[:], in_=warm_in[:], func=ACT.Abs_reciprocal_sqrt)
+            make_identity(nc, ident_bf[:])
+            make_identity(nc, ident_f32[:])
+
+        setup()
+        load_col(om_col, om)
+        load_col(nu_col, nu)
+        load_p_words()
+        load_col(b_col, b)
+        load_x(0)
+        load_x(1)
+        load_p_scales()
+        load_q(0)
+        load_q(1)
+        load_c()
+        load_x(2)
+        load_x(3)
+        load_q(2)
+        load_q(3)
+        spread_om()
+        permute_p_words()
+        x_interleave(0)
+        de_times_b()
+        lorentz_all()
+        x_quantize(0)
+        x_interleave(1)
+        permute_p_scales()
+        x_quantize(1)
+        for n in range(4):
+            q_transpose(n // 2, n % 2, 1 + n)
+            q_evict(n // 2, n % 2, 1 + n)
+        u_banks = [5, 6, 7, 0]
+        for j in range(4):
+            u_matmul(0, j, u_banks[j])
+        g_real(0)
+        g_real(1)
+        g_imag(0)
+        g_quantize(0)
+        g_imag(1)
+        x_interleave(2, on_scalar=True)
+        x_interleave(3, on_scalar=True)
+        q_quantize(0)
+        g_quantize(1)
+        q_quantize(1)
+        for part in range(2):
+            for j in range(4):
+                k_matmul(part, j, 1 + j)
+                k_evict(part, j, 1 + j)
+        for n in range(4):
+            q_transpose(2 + n // 2, n % 2, 1 + n)
+            q_evict(2 + n // 2, n % 2, 1 + n)
+        x_quantize(2)
+        x_quantize(3)
+        for j in range(4):
+            f_product(0, j, u_banks[j])
+        for j in range(4):
+            f_product(1, j, u_banks[j])
+            if j < 2:
+                u_matmul(1, j, u_banks[j])
+            if j == 0:
+                f_quantize(0, 0)
+        f_quantize(0, 1)
+        f_product(0, 0, u_banks[0])
+        def y_tile(pair, h, bk, v=False):
+            y_matmul(pair, h, bk)
+            y_evict(pair, h, bk, v)
+            y_store_h(pair, h)
+        def yt_tile(pair, h, bk, v=False):
+            yt_matmul(pair, h, bk)
+            yt_round(pair, h, bk, v)
+
+        y_tile(0, 0, 1)
+        u_matmul(1, 2, u_banks[2])
+        y_tile(0, 1, 2)
+        u_matmul(1, 3, u_banks[3])
+        y_tile(1, 0, 3)
+        y_tile(1, 1, 4)
+        f_product(0, 1, u_banks[1])
+        q_quantize(2)
+        f_product(0, 2, u_banks[2])
+        q_quantize(3)
+        y_tile(2, 0, 1)
+        y_tile(2, 1, 2)
+        y_tile(3, 0, 3)
+        y_tile(3, 1, 4)
+        f_product(0, 3, u_banks[3])
+        f_product(1, 0, u_banks[0])
+        f_quantize(1, 0)
+        for j in range(1, 4):
+            f_product(1, j, u_banks[j])
+        yt_tile(0, 0, 1)
+        yt_tile(0, 1, 2)
+        yt_tile(1, 0, 3)
+        yt_tile(1, 1, 4)
+        y_round(2)
+        f_quantize(1, 1)
+        y_round(3)
+        y_quantize(0)
+        y_tile(4, 0, 5)
+        y_tile(4, 1, 6)
+        y_transpose(2, 1)
+        y_transpose(3, 2)
+        y_quantize(1)
+        words_store(0, 2)
+        yt_evict(2, 1, True)
+        y_tile(5, 0, 7)
+        y_tile(5, 1, 0)
+        yt_evict(3, 2, True)
+        y_quantize(2)
+        y_round(4)
+        y_tile(6, 0, 3)
+        y_tile(6, 1, 4)
+        y_quantize(3)
+        words_store(2, 4)
+        scales_store(0, 4)
+        y_round(5)
+        y_transpose(4, 5)
+        yt_matmul(7, 0, 1)
+        yt_matmul(7, 1, 2)
+        y_transpose(5, 6)
+        yt_evict(4, 5)
+        y_round(6)
+        y_quantize(4)
+        yt_round(7, 0, 1)
+        y_transpose(6, 3)
+        y_matmul(7, 0, 7)
+        y_matmul(7, 1, 0)
+        yt_evict(5, 6, True)
+        yt_round(7, 1, 2)
+        y_quantize(5)
+        words_store(4, 6)
+        yt_evict(6, 3, True)
+        y_quantize(7)
+        y_evict(7, 0, 7)
+        y_store_h(7, 0)
+        y_quantize(6)
+        y_evict(7, 1, 0)
+        words_store(6, 8)
+        y_store_h(7, 1)
+        scales_store(4, 8)

@@ -72,11 +72,24 @@ def tile_cauchytransferfunctionfilter_x2_kernel(
         f_scale = tiles("f_scale", 4, [P, D], U8)
         y32 = tiles("y32", 8, [P, 2, D], F32)
         y_bf = tiles("y_bf", 3, [P, 2 * D], BF16)
-        yt_bf = tiles("yt_bf", 3, [P, 2 * D], BF16)
+        yt_bf = tiles("yt_bf", 4, [P, 2 * D], BF16)
         y_codes = tile("y_codes", [P, B * S], U32)
         y_scale = tile("y_scale", [P, B * S], U8)
 
-        def load_col(dst, vec):
+        x_grouped = [x_bf[0], x_bf[1], g_bf[1], g_bf[0]]
+        y_rounded = [q_bf[3][:, 0, :], q_bf[3][:, 1, :], q_bf[2][:, 0, :], q_bf[2][:, 1, :]]
+        y_rounded.extend([y_bf[0][:], y_bf[1][:], y_bf[2][:], y_bf[0][:]])
+
+        def copy_on(eng, dst, src):
+            if eng == "V":
+                nc.vector.tensor_copy(out=dst, in_=src)
+            elif eng == "A":
+                nc.scalar.copy(out=dst, in_=src)
+            else:
+                nc.gpsimd.tensor_scalar(out=dst, in0=src, scalar1=1.0, scalar2=1.0, op0=ALU.mult, op1=ALU.mult)
+
+        def load_col(name):
+            dst, vec = {"om": (om_col, om), "nu": (nu_col, nu), "b": (b_col, b)}[name]
             nc.sync.dma_start(out=dst[:], in_=vec.rearrange("(p t) -> p t", t=PACK))
 
         def load_x(i):
@@ -128,16 +141,15 @@ def tile_cauchytransferfunctionfilter_x2_kernel(
                 in_=psc_raw[:].rearrange("p g (m t) -> p t (g m)", t=PACK),
             )
 
-        def x_interleave(i, on_scalar=False):
-            dst = x_bf[i % 2][:].rearrange("p (c i) t -> p c t i", i=4)
-            src = x_raw[i][:].rearrange("p t (c i) -> p c t i", i=4)
-            if on_scalar:
-                nc.scalar.copy(out=dst, in_=src)
-            else:
-                nc.vector.tensor_copy(out=dst, in_=src)
+        def x_interleave(i, eng="V"):
+            copy_on(
+                eng,
+                x_grouped[i][:].rearrange("p (c i) t -> p c t i", i=4),
+                x_raw[i][:].rearrange("p t (c i) -> p c t i", i=4),
+            )
 
         def x_quantize(i):
-            quantize(x_codes[i][:], x_scale[i][:], flat(x_bf[i % 2]))
+            quantize(x_codes[i][:], x_scale[i][:], flat(x_grouped[i]))
 
         def spread_om():
             view = bank[0][:].bitcast(BF16)
@@ -198,10 +210,11 @@ def tile_cauchytransferfunctionfilter_x2_kernel(
                         words[:, 256 * h + u : 256 * (h + 1) : 2], ident_f32[:],
                     )
 
-        def q_evict(i, a, bk):
-            nc.scalar.copy(
-                out=q_bf[i][:, a, :].bitcast(F32).rearrange("p (s r) -> p s r", r=4),
-                in_=bank[bk][:].rearrange("p (r s) -> p s r", r=4),
+        def q_evict(i, a, bk, eng="A"):
+            copy_on(
+                eng,
+                q_bf[i][:, a, :].bitcast(F32).rearrange("p (s r) -> p s r", r=4),
+                bank[bk][:].rearrange("p (r s) -> p s r", r=4),
             )
 
         def q_quantize(i):
@@ -232,8 +245,8 @@ def tile_cauchytransferfunctionfilter_x2_kernel(
         def by_slot(bk):
             return bank[bk][:].rearrange("p (t a e) -> p e a t", t=4, e=4)
 
-        def k_evict(part, j, bk):
-            nc.scalar.copy(out=k_sb[part][:, j, :].rearrange("p (e a t) -> p e a t", e=4, t=4), in_=by_slot(bk))
+        def k_evict(part, j, bk, eng="A"):
+            copy_on(eng, k_sb[part][:, j, :].rearrange("p (e a t) -> p e a t", e=4, t=4), by_slot(bk))
 
         def f_product(part, j, bk):
             nc.vector.tensor_tensor(
@@ -257,15 +270,9 @@ def tile_cauchytransferfunctionfilter_x2_kernel(
                     start=(part == 0), stop=(part == 1),
                 )
 
-        def copy_on(on_vector, dst, src):
-            if on_vector:
-                nc.vector.tensor_copy(out=dst, in_=src)
-            else:
-                nc.scalar.copy(out=dst, in_=src)
-
-        def y_evict(pair, h, bk, on_vector=False):
+        def y_evict(pair, h, bk, eng="A"):
             copy_on(
-                on_vector,
+                eng,
                 y32[pair][:, h, :].rearrange("p (w e) -> p w e", e=4),
                 bank[bk][:].rearrange("p (e w) -> p w e", e=4),
             )
@@ -284,10 +291,10 @@ def tile_cauchytransferfunctionfilter_x2_kernel(
                         start=(part == 0), stop=(part == 1),
                     )
 
-        def yt_round(pair, h, bk, on_vector=False):
+        def yt_round(pair, h, bk, eng="A"):
             copy_on(
-                on_vector,
-                yt_bf[pair % 3][:, W * h : W * (h + 1)].rearrange("p (s t) -> p s t", t=4),
+                eng,
+                yt_bf[pair % 4][:, W * h : W * (h + 1)].rearrange("p (s t) -> p s t", t=4),
                 bank[bk][:].rearrange("p (t s) -> p s t", t=4),
             )
 
@@ -303,27 +310,35 @@ def tile_cauchytransferfunctionfilter_x2_kernel(
                 in_=y32[pair][:],
             )
 
-        def y_round(pair):
-            nc.vector.tensor_copy(
-                out=y_bf[pair % 3][:].rearrange("p (u w e) -> p u w e", u=2, e=2),
-                in_=flat(y32[pair]).rearrange("p (w u e) -> p u w e", u=2, e=2),
+        def y_round(pair, eng="V"):
+            copy_on(
+                eng,
+                y_rounded[pair].rearrange("p (u w e) -> p u w e", u=2, e=2),
+                flat(y32[pair]).rearrange("p (w u e) -> p u w e", u=2, e=2),
+            )
+
+        def y_cast(pair, h, bk, eng="A"):
+            copy_on(
+                eng,
+                y_rounded[pair].rearrange("p (u h w e) -> p h u w e", u=2, h=2, e=2)[:, h],
+                bank[bk][:].rearrange("p (u e w) -> p u w e", u=2, e=2),
             )
 
         def y_transpose(pair, bk):
-            words = y_bf[pair % 3][:].bitcast(F32)
+            words = y_rounded[pair].bitcast(F32)
             for r in range(4):
                 nc.tensor.transpose(bank[bk][:, P * r : P * (r + 1)], words[:, P * r : P * (r + 1)], ident_f32[:])
 
-        def yt_evict(pair, bk, on_vector=False):
+        def yt_evict(pair, bk, eng="A"):
             copy_on(
-                on_vector,
-                yt_bf[pair % 3][:].bitcast(F32).rearrange("p (w u) -> p w u", u=2),
+                eng,
+                yt_bf[pair % 4][:].bitcast(F32).rearrange("p (w u) -> p w u", u=2),
                 bank[bk][:].rearrange("p (u w) -> p w u", u=2),
             )
 
         def y_quantize(pair):
             sl = slice(256 * pair, 256 * (pair + 1))
-            quantize(y_codes[:, sl], y_scale[:, sl], yt_bf[pair % 3][:])
+            quantize(y_codes[:, sl], y_scale[:, sl], yt_bf[pair % 4][:])
 
         def words_store(lo, hi):
             sl = slice(256 * lo, 256 * hi)
@@ -348,138 +363,187 @@ def tile_cauchytransferfunctionfilter_x2_kernel(
             make_identity(nc, ident_f32[:])
 
         setup()
-        load_col(om_col, om)
-        load_col(nu_col, nu)
+        load_col('om')
         load_p_words()
-        load_col(b_col, b)
+        load_col('b')
+        spread_om()
+        load_col('nu')
+        permute_p_words()
+        load_q(1)
+        de_times_b()
         load_x(0)
         load_x(1)
         load_p_scales()
-        load_q(0)
-        load_q(1)
-        load_c()
-        load_x(2)
-        load_x(3)
-        load_q(2)
-        load_q(3)
-        spread_om()
-        permute_p_words()
-        x_interleave(0)
-        de_times_b()
-        lorentz_all()
-        x_quantize(0)
-        x_interleave(1)
+        x_interleave(0, 'V')
+        q_transpose(1, 0, 1)
+        q_transpose(1, 1, 3)
+        x_interleave(1, 'V')
         permute_p_scales()
+        load_q(3)
+        lorentz_all()
         x_quantize(1)
-        for n in range(4):
-            q_transpose(n // 2, n % 2, 1 + n)
-            q_evict(n // 2, n % 2, 1 + n)
-        u_banks = [5, 6, 7, 0]
-        for j in range(4):
-            u_matmul(0, j, u_banks[j])
+        q_transpose(3, 0, 6)
+        x_quantize(0)
+        q_evict(1, 0, 1, 'A')
+        load_q(2)
+        q_transpose(3, 1, 2)
+        q_transpose(2, 0, 0)
         g_real(0)
+        q_evict(1, 1, 3, 'A')
+        load_q(0)
+        u_matmul(0, 1, 7)
+        load_c()
+        q_evict(3, 0, 6, 'A')
         g_real(1)
-        g_imag(0)
-        g_quantize(0)
         g_imag(1)
-        x_interleave(2, on_scalar=True)
-        x_interleave(3, on_scalar=True)
-        q_quantize(0)
-        g_quantize(1)
+        g_quantize(0)
+        q_transpose(0, 0, 5)
+        load_x(3)
+        q_evict(0, 0, 5, 'A')
+        q_transpose(2, 1, 3)
+        q_evict(3, 1, 2, 'A')
+        g_imag(0)
+        q_transpose(0, 1, 6)
+        q_evict(0, 1, 6, 'A')
+        u_matmul(0, 3, 5)
         q_quantize(1)
-        for part in range(2):
-            for j in range(4):
-                k_matmul(part, j, 1 + j)
-                k_evict(part, j, 1 + j)
-        for n in range(4):
-            q_transpose(2 + n // 2, n % 2, 1 + n)
-            q_evict(2 + n // 2, n % 2, 1 + n)
+        q_evict(2, 1, 3, 'A')
+        u_matmul(0, 2, 1)
+        q_evict(2, 0, 0, 'A')
+        g_quantize(1)
+        k_matmul(0, 2, 6)
+        k_evict(0, 2, 6, 'A')
+        k_matmul(0, 3, 3)
+        k_matmul(0, 1, 4)
+        k_matmul(1, 0, 6)
+        k_evict(0, 3, 3, 'A')
+        k_matmul(1, 2, 2)
+        k_evict(0, 1, 4, 'A')
+        u_matmul(0, 0, 3)
+        k_evict(1, 0, 6, 'A')
+        k_matmul(0, 0, 0)
+        q_quantize(0)
+        k_evict(1, 2, 2, 'A')
+        k_evict(0, 0, 0, 'A')
+        k_matmul(1, 1, 6)
+        load_x(2)
+        f_product(0, 3, 5)
+        f_product(0, 1, 7)
+        f_product(0, 2, 1)
+        k_matmul(1, 3, 0)
+        k_evict(1, 1, 6, 'A')
+        x_interleave(2, 'G')
+        f_product(1, 2, 1)
+        f_product(0, 0, 3)
+        f_product(1, 0, 3)
+        k_evict(1, 3, 0, 'A')
+        f_quantize(0, 0)
+        f_product(1, 1, 7)
+        f_product(1, 3, 5)
+        f_quantize(0, 1)
+        x_interleave(3, 'A')
+        y_matmul(0, 1, 1)
         x_quantize(2)
         x_quantize(3)
-        for j in range(4):
-            f_product(0, j, u_banks[j])
-        for j in range(4):
-            f_product(1, j, u_banks[j])
-            if j < 2:
-                u_matmul(1, j, u_banks[j])
-            if j == 0:
-                f_quantize(0, 0)
-        f_quantize(0, 1)
-        f_product(0, 0, u_banks[0])
-        def y_tile(pair, h, bk, v=False):
-            y_matmul(pair, h, bk)
-            y_evict(pair, h, bk, v)
-            y_store_h(pair, h)
-        def yt_tile(pair, h, bk, v=False):
-            yt_matmul(pair, h, bk)
-            yt_round(pair, h, bk, v)
-
-        y_tile(0, 0, 1)
-        u_matmul(1, 2, u_banks[2])
-        y_tile(0, 1, 2)
-        u_matmul(1, 3, u_banks[3])
-        y_tile(1, 0, 3)
-        y_tile(1, 1, 4)
-        f_product(0, 1, u_banks[1])
         q_quantize(2)
-        f_product(0, 2, u_banks[2])
+        y_evict(0, 1, 1, 'A')
+        y_matmul(1, 1, 7)
+        y_matmul(0, 0, 5)
+        u_matmul(1, 3, 0)
         q_quantize(3)
-        y_tile(2, 0, 1)
-        y_tile(2, 1, 2)
-        y_tile(3, 0, 3)
-        y_tile(3, 1, 4)
-        f_product(0, 3, u_banks[3])
-        f_product(1, 0, u_banks[0])
+        f_product(1, 3, 0)
+        y_evict(0, 0, 5, 'A')
+        u_matmul(1, 0, 6)
+        y_evict(1, 1, 7, 'A')
+        u_matmul(1, 1, 4)
+        y_matmul(1, 0, 1)
+        f_product(0, 3, 0)
+        y_evict(1, 0, 1, 'A')
+        f_product(0, 0, 6)
+        u_matmul(1, 2, 2)
+        y_round(0, 'G')
+        f_product(0, 1, 4)
+        y_matmul(3, 0, 5)
+        y_evict(3, 0, 5, 'A')
+        y_matmul(2, 0, 1)
+        y_store_h(0, 1)
+        f_product(1, 0, 6)
+        y_evict(2, 0, 1, 'A')
+        y_store_h(1, 0)
+        y_matmul(3, 1, 0)
+        f_product(0, 2, 2)
+        y_evict(3, 1, 0, 'A')
+        y_round(1, 'G')
+        f_product(1, 1, 4)
+        y_round(3, 'G')
+        y_matmul(2, 1, 6)
+        f_product(1, 2, 2)
         f_quantize(1, 0)
-        for j in range(1, 4):
-            f_product(1, j, u_banks[j])
-        yt_tile(0, 0, 1)
-        yt_tile(0, 1, 2)
-        yt_tile(1, 0, 3)
-        yt_tile(1, 1, 4)
-        y_round(2)
+        y_transpose(1, 3)
         f_quantize(1, 1)
-        y_round(3)
-        y_quantize(0)
-        y_tile(4, 0, 5)
-        y_tile(4, 1, 6)
-        y_transpose(2, 1)
-        y_transpose(3, 2)
+        y_transpose(0, 2)
+        y_evict(2, 1, 6, 'A')
+        y_store_h(3, 0)
+        y_store_h(2, 0)
+        y_store_h(1, 1)
+        yt_evict(1, 3, 'V')
+        y_matmul(6, 0, 0)
+        y_matmul(6, 1, 7)
+        y_cast(2, 0, 1)
+        y_evict(6, 0, 0, 'V')
+        y_matmul(4, 1, 4)
+        y_matmul(4, 0, 3)
+        yt_evict(0, 2, 'A')
         y_quantize(1)
+        y_store_h(0, 0)
+        y_cast(2, 1, 6)
+        y_matmul(7, 1, 6)
+        y_matmul(5, 1, 0)
+        y_evict(6, 1, 7, 'A')
+        y_round(6, 'V')
+        y_store_h(2, 1)
+        y_matmul(5, 0, 1)
+        y_quantize(0)
+        y_evict(7, 1, 6, 'V')
+        y_store_h(6, 0)
+        y_transpose(3, 7)
+        y_evict(4, 1, 4, 'A')
+        y_store_h(3, 1)
+        y_evict(4, 0, 3, 'A')
+        yt_evict(3, 7, 'A')
+        y_evict(5, 1, 0, 'V')
+        y_store_h(6, 1)
+        y_transpose(2, 0)
+        y_evict(5, 0, 1, 'V')
         words_store(0, 2)
-        yt_evict(2, 1, True)
-        y_tile(5, 0, 7)
-        y_tile(5, 1, 0)
-        yt_evict(3, 2, True)
-        y_quantize(2)
-        y_round(4)
-        y_tile(6, 0, 3)
-        y_tile(6, 1, 4)
-        y_quantize(3)
-        words_store(2, 4)
-        scales_store(0, 4)
-        y_round(5)
-        y_transpose(4, 5)
-        yt_matmul(7, 0, 1)
-        yt_matmul(7, 1, 2)
-        y_transpose(5, 6)
-        yt_evict(4, 5)
-        y_round(6)
-        y_quantize(4)
-        yt_round(7, 0, 1)
-        y_transpose(6, 3)
-        y_matmul(7, 0, 7)
-        y_matmul(7, 1, 0)
-        yt_evict(5, 6, True)
-        yt_round(7, 1, 2)
-        y_quantize(5)
-        words_store(4, 6)
-        yt_evict(6, 3, True)
-        y_quantize(7)
-        y_evict(7, 0, 7)
-        y_store_h(7, 0)
-        y_quantize(6)
-        y_evict(7, 1, 0)
-        words_store(6, 8)
+        y_store_h(4, 1)
+        y_round(5, 'V')
+        y_store_h(4, 0)
+        y_matmul(7, 0, 2)
+        yt_evict(2, 0, 'A')
+        y_evict(7, 0, 2, 'A')
+        y_round(4, 'G')
+        y_transpose(4, 6)
         y_store_h(7, 1)
+        y_quantize(3)
+        yt_evict(4, 6, 'A')
+        y_transpose(5, 4)
+        y_quantize(2)
+        y_round(7, 'V')
+        y_transpose(6, 0)
+        y_quantize(4)
+        yt_evict(6, 0, 'V')
+        yt_evict(5, 4, 'A')
+        y_store_h(5, 0)
+        y_transpose(7, 1)
+        y_quantize(5)
+        y_store_h(5, 1)
+        scales_store(0, 4)
+        yt_evict(7, 1, 'A')
+        y_store_h(7, 0)
+        words_store(2, 4)
+        y_quantize(6)
+        words_store(4, 6)
+        y_quantize(7)
+        words_store(6, 8)
         scales_store(4, 8)

@@ -47,7 +47,7 @@ def tile_cauchytransferfunctionfilter_x2_kernel(
         b_col = tile("b_col", [P, PACK], BF16)
         om_row = tile("om_row", [P, M], BF16)
         dist = tile("dist", [P, PACK, M], F32)
-        lorentz = tile("lorentz", [P, M, PACK], F32)
+        half_b = tile("half_b", [P, PACK], F32)
         de_b = tile("de_b", [P, PACK, M], F32)
         g_bf = tiles("g_bf", 2, [P, M, PACK], BF16)
         g_codes = tiles("g_codes", 2, [P, M], U32)
@@ -58,27 +58,27 @@ def tile_cauchytransferfunctionfilter_x2_kernel(
         psc = tile("psc", [P, PACK, 2, P], U8)
         cw = tile("cw", [P, 2 * D], U8)
         csc = tile("csc", [P, D], U8)
-        x_raw = tiles("x_raw", 4, [P, PACK, D], BF16)
-        x_bf = tiles("x_bf", 2, [P, D, PACK], BF16)
-        x_codes = tiles("x_codes", 4, [P, D], U32)
-        x_scale = tiles("x_scale", 4, [P, D], U8)
+        x_raw = tile("x_raw", [P, 4, PACK * D], BF16)
+        x_bf = tile("x_bf", [P, 2, PACK * D], BF16)
+        x_codes = tile("x_codes", [P, 4, D], U32)
+        x_scale = tile("x_scale", [P, 4, D], U8)
         q_raw = tiles("q_raw", 4, [P, 2, 2 * M], BF16)
-        q_bf = tiles("q_bf", 4, [P, 2, 4 * 2 * P], BF16)
-        q_codes = tiles("q_codes", 4, [P, W], U32)
-        q_scale = tiles("q_scale", 4, [P, W], U8)
-        k_sb = tiles("k_sb", 2, [P, 4, W], F32)
-        f_bf = tiles("f_bf", 2, [P, D, PACK], BF16)
-        f_codes = tiles("f_codes", 4, [P, D], U32)
-        f_scale = tiles("f_scale", 4, [P, D], U8)
-        y32 = tiles("y32", 8, [P, 2, D], F32)
-        y_bf = tiles("y_bf", 3, [P, 2 * D], BF16)
-        yt_bf = tiles("yt_bf", 4, [P, 2 * D], BF16)
+        q_bf = tile("q_bf", [P, 4, 2, 2 * W], BF16)
+        q_codes = tile("q_codes", [P, 4, W], U32)
+        q_scale = tile("q_scale", [P, 4, W], U8)
+        u_sb = tiles("u_sb", 2, [P, 4, W], F32)
+        f_bf = tile("f_bf", [P, 2, PACK * D], BF16)
+        f_codes = tile("f_codes", [P, 4, D], U32)
+        f_scale = tile("f_scale", [P, 4, D], U8)
+        y32 = tile("y32", [P, 8, 2, D], F32)
+        y_bf = tile("y_bf", [P, 4, 2 * D], BF16)
+        yt_bf = tile("yt_bf", [P, 4, 2 * D], BF16)
         y_codes = tile("y_codes", [P, B * S], U32)
         y_scale = tile("y_scale", [P, B * S], U8)
 
-        x_grouped = [x_bf[0], x_bf[1], g_bf[1], g_bf[0]]
-        y_rounded = [q_bf[3][:, 0, :], q_bf[3][:, 1, :], q_bf[2][:, 0, :], q_bf[2][:, 1, :]]
-        y_rounded.extend([y_bf[0][:], y_bf[1][:], y_bf[2][:], y_bf[0][:]])
+        x_grouped = [x_bf[:], x_raw[:, 0:2, :]]
+        y_rounded = [q_bf[:, 0], q_bf[:, 1], y_bf[:, 0:2, :], y_bf[:, 2:4, :]]
+        y_words = {}
 
         def copy_on(eng, dst, src):
             if eng == "V":
@@ -95,7 +95,7 @@ def tile_cauchytransferfunctionfilter_x2_kernel(
         def load_x(i):
             bi, g = divmod(i, 2)
             nc.sync.dma_start(
-                out=x_raw[i][:], in_=x[bi, W * g : W * (g + 1), :].rearrange("(p j) d -> p j d", j=PACK)
+                out=x_raw[:, i, :], in_=x[bi, W * g : W * (g + 1), :].rearrange("(p j) d -> p (j d)", j=PACK)
             )
 
         def load_q(i):
@@ -126,8 +126,8 @@ def tile_cauchytransferfunctionfilter_x2_kernel(
         def quantize(codes, scale, src):
             nc.vector.quantize_mx(out=codes.bitcast(FP8X4), scales=scale, in_=src)
 
-        def flat(t):
-            return t[:].rearrange("p a b -> p (a b)")
+        def flat(ap):
+            return ap.rearrange("p a b -> p (a b)")
 
         def permute_p_words():
             nc.vector.tensor_copy(
@@ -144,12 +144,16 @@ def tile_cauchytransferfunctionfilter_x2_kernel(
         def x_interleave(i, eng="V"):
             copy_on(
                 eng,
-                x_grouped[i][:].rearrange("p (c i) t -> p c t i", i=4),
-                x_raw[i][:].rearrange("p t (c i) -> p c t i", i=4),
+                x_grouped[i // 2][:, i % 2, :].rearrange("p (c i t) -> p c t i", i=4, t=4),
+                x_raw[:, i, :].rearrange("p (t c i) -> p c t i", i=4, t=4),
             )
 
         def x_quantize(i):
-            quantize(x_codes[i][:], x_scale[i][:], flat(x_grouped[i]))
+            quantize(x_codes[:, i, :], x_scale[:, i, :], x_grouped[i // 2][:, i % 2, :])
+
+        def x_quantize2(bi):
+            sl = slice(2 * bi, 2 * bi + 2)
+            quantize(flat(x_codes[:, sl, :]), flat(x_scale[:, sl, :]), flat(x_grouped[bi]))
 
         def spread_om():
             view = bank[0][:].bitcast(BF16)
@@ -162,44 +166,47 @@ def tile_cauchytransferfunctionfilter_x2_kernel(
         def cols(half):
             return slice(256 * half, 256 * (half + 1))
 
-        def lorentz_all():
-            for half in range(2):
-                for t in range(PACK):
-                    nc.scalar.activation(
-                        out=dist[:, t, cols(half)], in_=om_row[:, cols(half)], func=ACT.Square,
-                        bias=nu_col[:, t : t + 1], scale=-1.0,
-                    )
+        def lorentz4():
+            for t in range(PACK):
+                nc.scalar.activation(
+                    out=dist[:, t, :], in_=om_row[:], func=ACT.Square, bias=nu_col[:, t : t + 1], scale=-1.0
+                )
             for half in range(2):
                 nc.scalar.activation(
                     out=dist[:, :, cols(half)], in_=dist[:, :, cols(half)], func=ACT.Abs_reciprocal_sqrt, bias=0.25
                 )
             for half in range(2):
                 nc.scalar.activation(
-                    out=lorentz[:, cols(half), :], in_=dist[:, :, cols(half)].rearrange("p t m -> p m t"),
-                    func=ACT.Square,
+                    out=dist[:, :, cols(half)], in_=dist[:, :, cols(half)], func=ACT.Square
                 )
 
         def de_times_b():
+            nc.gpsimd.tensor_scalar(
+                out=half_b[:], in0=b_col[:], scalar1=0.5, scalar2=1.0, op0=ALU.mult, op1=ALU.mult
+            )
             for t in range(PACK):
                 nc.vector.tensor_scalar(
                     out=de_b[:, t, :], in0=om_row[:], scalar1=nu_col[:, t : t + 1], scalar2=b_col[:, t : t + 1],
                     op0=ALU.subtract, op1=ALU.mult,
                 )
 
-        def g_real(half):
-            nc.vector.scalar_tensor_tensor(
-                out=g_bf[0][:, cols(half), :], in0=lorentz[:, cols(half), :], scalar=0.5,
-                in1=b_col[:].unsqueeze(1).to_broadcast([P, 256, PACK]), op0=ALU.mult, op1=ALU.mult,
+        def by_run(ap):
+            return ap.rearrange("p t (c i) -> p c t i", i=4)
+
+        def g_product(part, half, factor):
+            nc.vector.tensor_tensor(
+                out=g_bf[part][:, cols(half), :].rearrange("p (c i) t -> p c t i", i=4),
+                in0=by_run(dist[:, :, cols(half)]), in1=factor, op=ALU.mult,
             )
+
+        def g_real(half):
+            g_product(0, half, half_b[:].unsqueeze(1).unsqueeze(3).to_broadcast([P, 64, PACK, 4]))
 
         def g_imag(half):
-            nc.vector.tensor_tensor(
-                out=g_bf[1][:, cols(half), :], in0=lorentz[:, cols(half), :],
-                in1=de_b[:, :, cols(half)].rearrange("p t m -> p m t"), op=ALU.mult,
-            )
+            g_product(1, half, by_run(de_b[:, :, cols(half)]))
 
         def g_quantize(part):
-            quantize(g_codes[part][:], g_scale[part][:], flat(g_bf[part]))
+            quantize(g_codes[part][:], g_scale[part][:], flat(g_bf[part][:]))
 
         def q_transpose(i, a, bk):
             words = q_raw[i][:, a, :].bitcast(F32)
@@ -213,12 +220,18 @@ def tile_cauchytransferfunctionfilter_x2_kernel(
         def q_evict(i, a, bk, eng="A"):
             copy_on(
                 eng,
-                q_bf[i][:, a, :].bitcast(F32).rearrange("p (s r) -> p s r", r=4),
+                q_bf[:, i, a, :].bitcast(F32).rearrange("p (s r) -> p s r", r=4),
                 bank[bk][:].rearrange("p (r s) -> p s r", r=4),
             )
 
         def q_quantize(i):
-            quantize(q_codes[i][:], q_scale[i][:], flat(q_bf[i]))
+            quantize(q_codes[:, i, :], q_scale[:, i, :], flat(q_bf[:, i]))
+
+        def q_quantize2(half):
+            sl = slice(2 * half, 2 * half + 2)
+            quantize(
+                flat(q_codes[:, sl, :]), flat(q_scale[:, sl, :]), q_bf[:, sl].rearrange("p c a w -> p (c a w)")
+            )
 
         def u_matmul(bi, j, bk):
             for t in range(PACK):
@@ -226,8 +239,8 @@ def tile_cauchytransferfunctionfilter_x2_kernel(
                     nc.tensor.matmul_mx(
                         out=bank[bk][:, P * t : P * (t + 1)],
                         lhsT=pw[:, t, g, :].bitcast(FP4X4), lhsT_scale=psc[:, t, g, :],
-                        rhs=x_codes[2 * bi + g][:, P * j : P * (j + 1)].bitcast(FP8X4),
-                        rhs_scale=x_scale[2 * bi + g][:, P * j : P * (j + 1)],
+                        rhs=x_codes[:, 2 * bi + g, P * j : P * (j + 1)].bitcast(FP8X4),
+                        rhs_scale=x_scale[:, 2 * bi + g, P * j : P * (j + 1)],
                         start=(g == 0), stop=(g == 1),
                     )
 
@@ -245,35 +258,42 @@ def tile_cauchytransferfunctionfilter_x2_kernel(
         def by_slot(bk):
             return bank[bk][:].rearrange("p (t a e) -> p e a t", t=4, e=4)
 
-        def k_evict(part, j, bk, eng="A"):
-            copy_on(eng, k_sb[part][:, j, :].rearrange("p (e a t) -> p e a t", e=4, t=4), by_slot(bk))
+        def u_evict(bi, j, bk, eng="A"):
+            copy_on(eng, u_sb[bi][:, j, :].rearrange("p (e a t) -> p e a t", e=4, t=4), by_slot(bk))
 
-        def f_product(part, j, bk):
+        def f_mul(bi, part, j, bk):
             nc.vector.tensor_tensor(
-                out=f_bf[part][:].rearrange("p (e w) t -> p e w t", e=4)[:, :, 32 * j : 32 * (j + 1), :],
+                out=f_bf[:, part, :].rearrange("p (e w t) -> p e w t", e=4, t=4)[:, :, 32 * j : 32 * (j + 1), :],
                 in0=by_slot(bk),
-                in1=k_sb[part][:, j, :].rearrange("p (e a t) -> p e a t", e=4, t=4), op=ALU.mult,
+                in1=u_sb[bi][:, j, :].rearrange("p (e a t) -> p e a t", e=4, t=4), op=ALU.mult,
             )
 
         def f_quantize(bi, part):
-            quantize(f_codes[2 * bi + part][:], f_scale[2 * bi + part][:], flat(f_bf[part]))
+            quantize(f_codes[:, 2 * bi + part, :], f_scale[:, 2 * bi + part, :], f_bf[:, part, :])
 
-        def y_matmul(pair, h, bk):
+        def f_quantize2(bi):
+            sl = slice(2 * bi, 2 * bi + 2)
+            quantize(flat(f_codes[:, sl, :]), flat(f_scale[:, sl, :]), flat(f_bf[:]))
+
+        def y_pass(pair, h, bk, part):
             bi, blk = divmod(pair, 4)
             half, a = divmod(blk, 2)
             sl = slice(256 * a + P * h, 256 * a + P * (h + 1))
-            for part in range(2):
-                nc.tensor.matmul_mx(
-                    out=bank[bk][:],
-                    lhsT=q_codes[2 * half + part][:, sl].bitcast(FP8X4), lhsT_scale=q_scale[2 * half + part][:, sl],
-                    rhs=f_codes[2 * bi + part][:].bitcast(FP8X4), rhs_scale=f_scale[2 * bi + part][:],
-                    start=(part == 0), stop=(part == 1),
-                )
+            nc.tensor.matmul_mx(
+                out=bank[bk][:],
+                lhsT=q_codes[:, 2 * half + part, sl].bitcast(FP8X4), lhsT_scale=q_scale[:, 2 * half + part, sl],
+                rhs=f_codes[:, 2 * bi + part, :].bitcast(FP8X4), rhs_scale=f_scale[:, 2 * bi + part, :],
+                start=(part == 0), stop=(part == 1),
+            )
+
+        def y_matmul(pair, h, bk):
+            y_pass(pair, h, bk, 0)
+            y_pass(pair, h, bk, 1)
 
         def y_evict(pair, h, bk, eng="A"):
             copy_on(
                 eng,
-                y32[pair][:, h, :].rearrange("p (w e) -> p w e", e=4),
+                y32[:, pair, h, :].rearrange("p (w e) -> p w e", e=4),
                 bank[bk][:].rearrange("p (e w) -> p w e", e=4),
             )
 
@@ -286,59 +306,72 @@ def tile_cauchytransferfunctionfilter_x2_kernel(
                 for part in range(2):
                     nc.tensor.matmul_mx(
                         out=bank[bk][:, ch],
-                        lhsT=f_codes[2 * bi + part][:, ch].bitcast(FP8X4), lhsT_scale=f_scale[2 * bi + part][:, ch],
-                        rhs=q_codes[2 * half + part][:, sl].bitcast(FP8X4), rhs_scale=q_scale[2 * half + part][:, sl],
+                        lhsT=f_codes[:, 2 * bi + part, ch].bitcast(FP8X4), lhsT_scale=f_scale[:, 2 * bi + part, ch],
+                        rhs=q_codes[:, 2 * half + part, sl].bitcast(FP8X4), rhs_scale=q_scale[:, 2 * half + part, sl],
                         start=(part == 0), stop=(part == 1),
                     )
 
         def yt_round(pair, h, bk, eng="A"):
             copy_on(
                 eng,
-                yt_bf[pair % 4][:, W * h : W * (h + 1)].rearrange("p (s t) -> p s t", t=4),
+                yt_bf[:, pair % 4, W * h : W * (h + 1)].rearrange("p (s t) -> p s t", t=4),
                 bank[bk][:].rearrange("p (t s) -> p s t", t=4),
             )
 
         def y_store_h(pair, h):
             bi, blk = divmod(pair, 4)
             lo = 256 * blk + P * h
-            nc.sync.dma_start(out=out_0[bi, lo : lo + P, :], in_=y32[pair][:, h, :])
-
-        def y_store(pair):
-            bi, blk = divmod(pair, 4)
-            nc.sync.dma_start(
-                out=out_0[bi, 256 * blk : 256 * (blk + 1), :].rearrange("(h p) d -> p h d", h=2),
-                in_=y32[pair][:],
-            )
+            nc.sync.dma_start(out=out_0[bi, lo : lo + P, :], in_=y32[:, pair, h, :])
 
         def y_round(pair, eng="V"):
+            dst = y_rounded[pair // 2][:, pair % 2, :]
             copy_on(
                 eng,
-                y_rounded[pair].rearrange("p (u w e) -> p u w e", u=2, e=2),
-                flat(y32[pair]).rearrange("p (w u e) -> p u w e", u=2, e=2),
+                dst.rearrange("p (u w e) -> p u w e", u=2, e=2),
+                flat(y32[:, pair]).rearrange("p (w u e) -> p u w e", u=2, e=2),
             )
+            y_words[pair] = dst.bitcast(F32).rearrange("p (u w) -> p u w", u=2)
+
+        def y_round2(k):
+            dst = flat(y_rounded[k])
+            nc.vector.tensor_copy(
+                out=dst.rearrange("p (u w e) -> p u w e", u=2, e=2),
+                in_=y32[:, 2 * k : 2 * k + 2].rearrange("p a h (w u e) -> p u (a h w) e", u=2, e=2),
+            )
+            for a in range(2):
+                y_words[2 * k + a] = dst.bitcast(F32).rearrange("p (u w) -> p u w", u=2)[:, :, 256 * a : 256 * (a + 1)]
 
         def y_cast(pair, h, bk, eng="A"):
+            dst = y_rounded[pair // 2][:, pair % 2, :]
             copy_on(
                 eng,
-                y_rounded[pair].rearrange("p (u h w e) -> p h u w e", u=2, h=2, e=2)[:, h],
+                dst.rearrange("p (u h w e) -> p h u w e", u=2, h=2, e=2)[:, h],
                 bank[bk][:].rearrange("p (u e w) -> p u w e", u=2, e=2),
             )
+            y_words[pair] = dst.bitcast(F32).rearrange("p (u w) -> p u w", u=2)
 
         def y_transpose(pair, bk):
-            words = y_rounded[pair].bitcast(F32)
-            for r in range(4):
-                nc.tensor.transpose(bank[bk][:, P * r : P * (r + 1)], words[:, P * r : P * (r + 1)], ident_f32[:])
+            for u in range(2):
+                for h in range(2):
+                    nc.tensor.transpose(
+                        bank[bk][:, P * (2 * u + h) : P * (2 * u + h + 1)],
+                        y_words[pair][:, u, P * h : P * (h + 1)], ident_f32[:],
+                    )
 
         def yt_evict(pair, bk, eng="A"):
             copy_on(
                 eng,
-                yt_bf[pair % 4][:].bitcast(F32).rearrange("p (w u) -> p w u", u=2),
+                yt_bf[:, pair % 4, :].bitcast(F32).rearrange("p (w u) -> p w u", u=2),
                 bank[bk][:].rearrange("p (u w) -> p w u", u=2),
             )
 
         def y_quantize(pair):
             sl = slice(256 * pair, 256 * (pair + 1))
-            quantize(y_codes[:, sl], y_scale[:, sl], yt_bf[pair % 4][:])
+            quantize(y_codes[:, sl], y_scale[:, sl], yt_bf[:, pair % 4, :])
+
+        def y_quantize2(k):
+            sl = slice(W * k, W * (k + 1))
+            quantize(y_codes[:, sl], y_scale[:, sl], flat(yt_bf[:, 2 * (k % 2) : 2 * (k % 2) + 2, :]))
 
         def words_store(lo, hi):
             sl = slice(256 * lo, 256 * hi)
@@ -349,14 +382,26 @@ def tile_cauchytransferfunctionfilter_x2_kernel(
         def scales_store(lo, hi):
             sl = slice(256 * lo, 256 * hi)
             for quad in range(4):
-                nc.sync.dma_start(
+                (nc.sync if lo == 0 else nc.scalar).dma_start(
                     out=out_2[0, 4 * quad : 4 * quad + 4, sl].bitcast(I32),
                     in_=y_scale[32 * quad : 32 * quad + 4, sl].bitcast(I32),
                 )
 
+        def y_out(pair, h, bk, eng="A"):
+            y_evict(pair, h, bk, eng)
+            y_store_h(pair, h)
+
+        def planes2(k):
+            y_quantize2(k)
+            words_store(2 * k, 2 * k + 2)
+
+        def planes1(pair):
+            y_quantize(pair)
+            words_store(pair, pair + 1)
+
         def setup():
             nc.vector.memset(warm_in[:], 1.0)
-            nc.vector.memset(flat(psc_raw).bitcast(I32), 0)
+            nc.vector.memset(flat(psc_raw[:]).bitcast(I32), 0)
             nc.vector.memset(csc[:].bitcast(I32), 0)
             nc.scalar.activation(out=warm_out[:], in_=warm_in[:], func=ACT.Abs_reciprocal_sqrt)
             make_identity(nc, ident_bf[:])
@@ -365,185 +410,164 @@ def tile_cauchytransferfunctionfilter_x2_kernel(
         setup()
         load_col('om')
         load_p_words()
-        load_col('b')
-        spread_om()
         load_col('nu')
-        permute_p_words()
-        load_q(1)
-        de_times_b()
         load_x(0)
-        load_x(1)
-        load_p_scales()
+        permute_p_words()
         x_interleave(0, 'V')
-        q_transpose(1, 0, 1)
-        q_transpose(1, 1, 3)
+        spread_om()
+        load_col('b')
+        load_x(1)
         x_interleave(1, 'V')
+        load_p_scales()
         permute_p_scales()
-        load_q(3)
-        lorentz_all()
-        x_quantize(1)
-        q_transpose(3, 0, 6)
-        x_quantize(0)
-        q_evict(1, 0, 1, 'A')
+        x_quantize2(0)
         load_q(2)
-        q_transpose(3, 1, 2)
-        q_transpose(2, 0, 0)
-        g_real(0)
-        q_evict(1, 1, 3, 'A')
-        load_q(0)
-        u_matmul(0, 1, 7)
+        lorentz4()
+        q_transpose(2, 0, 5)
         load_c()
-        q_evict(3, 0, 6, 'A')
-        g_real(1)
-        g_imag(1)
-        g_quantize(0)
-        q_transpose(0, 0, 5)
-        load_x(3)
-        q_evict(0, 0, 5, 'A')
-        q_transpose(2, 1, 3)
-        q_evict(3, 1, 2, 'A')
-        g_imag(0)
-        q_transpose(0, 1, 6)
-        q_evict(0, 1, 6, 'A')
-        u_matmul(0, 3, 5)
-        q_quantize(1)
-        q_evict(2, 1, 3, 'A')
-        u_matmul(0, 2, 1)
-        q_evict(2, 0, 0, 'A')
-        g_quantize(1)
-        k_matmul(0, 2, 6)
-        k_evict(0, 2, 6, 'A')
-        k_matmul(0, 3, 3)
-        k_matmul(0, 1, 4)
-        k_matmul(1, 0, 6)
-        k_evict(0, 3, 3, 'A')
-        k_matmul(1, 2, 2)
-        k_evict(0, 1, 4, 'A')
-        u_matmul(0, 0, 3)
-        k_evict(1, 0, 6, 'A')
-        k_matmul(0, 0, 0)
-        q_quantize(0)
-        k_evict(1, 2, 2, 'A')
-        k_evict(0, 0, 0, 'A')
-        k_matmul(1, 1, 6)
+        de_times_b()
+        q_transpose(2, 1, 2)
+        g_real(0)
         load_x(2)
-        f_product(0, 3, 5)
-        f_product(0, 1, 7)
-        f_product(0, 2, 1)
-        k_matmul(1, 3, 0)
-        k_evict(1, 1, 6, 'A')
-        x_interleave(2, 'G')
-        f_product(1, 2, 1)
-        f_product(0, 0, 3)
-        f_product(1, 0, 3)
-        k_evict(1, 3, 0, 'A')
-        f_quantize(0, 0)
-        f_product(1, 1, 7)
-        f_product(1, 3, 5)
-        f_quantize(0, 1)
+        u_matmul(0, 3, 1)
+        q_evict(2, 0, 5, 'A')
+        g_real(1)
+        u_evict(0, 3, 1, 'A')
+        u_matmul(0, 1, 4)
+        load_q(0)
+        u_matmul(0, 2, 6)
+        g_imag(1)
+        u_evict(0, 2, 6, 'A')
+        q_evict(2, 1, 2, 'A')
+        q_transpose(0, 0, 3)
+        u_matmul(0, 0, 7)
+        load_q(1)
+        g_quantize(0)
+        q_transpose(1, 0, 6)
+        u_evict(0, 1, 4, 'A')
+        q_evict(0, 0, 3, 'A')
+        load_x(3)
+        k_matmul(0, 0, 1)
+        k_matmul(0, 2, 3)
+        u_evict(0, 0, 7, 'A')
+        x_interleave(2, 'A')
+        g_imag(0)
+        f_mul(0, 0, 0, 1)
         x_interleave(3, 'A')
-        y_matmul(0, 1, 1)
-        x_quantize(2)
-        x_quantize(3)
-        q_quantize(2)
-        y_evict(0, 1, 1, 'A')
-        y_matmul(1, 1, 7)
-        y_matmul(0, 0, 5)
-        u_matmul(1, 3, 0)
-        q_quantize(3)
-        f_product(1, 3, 0)
-        y_evict(0, 0, 5, 'A')
-        u_matmul(1, 0, 6)
-        y_evict(1, 1, 7, 'A')
-        u_matmul(1, 1, 4)
-        y_matmul(1, 0, 1)
-        f_product(0, 3, 0)
-        y_evict(1, 0, 1, 'A')
-        f_product(0, 0, 6)
-        u_matmul(1, 2, 2)
-        y_round(0, 'G')
-        f_product(0, 1, 4)
-        y_matmul(3, 0, 5)
-        y_evict(3, 0, 5, 'A')
-        y_matmul(2, 0, 1)
-        y_store_h(0, 1)
-        f_product(1, 0, 6)
-        y_evict(2, 0, 1, 'A')
-        y_store_h(1, 0)
-        y_matmul(3, 1, 0)
-        f_product(0, 2, 2)
-        y_evict(3, 1, 0, 'A')
-        y_round(1, 'G')
-        f_product(1, 1, 4)
-        y_round(3, 'G')
-        y_matmul(2, 1, 6)
-        f_product(1, 2, 2)
+        k_matmul(0, 1, 5)
+        g_quantize(1)
+        f_mul(0, 0, 2, 3)
+        k_matmul(1, 2, 2)
+        k_matmul(0, 3, 1)
+        load_q(3)
+        k_matmul(1, 1, 4)
+        f_mul(0, 0, 1, 5)
+        k_matmul(1, 3, 7)
+        f_mul(0, 1, 2, 2)
+        f_mul(0, 0, 3, 1)
+        f_mul(0, 1, 3, 7)
+        q_evict(1, 0, 6, 'A')
+        k_matmul(1, 0, 5)
+        f_mul(0, 1, 1, 4)
+        q_transpose(3, 0, 3)
+        q_transpose(1, 1, 2)
+        q_transpose(0, 1, 1)
+        q_transpose(3, 1, 7)
+        k_matmul(0, 0, 4)
+        q_evict(3, 0, 3, 'A')
+        x_quantize2(1)
+        q_evict(3, 1, 7, 'A')
+        k_matmul(1, 3, 0)
+        q_evict(0, 1, 1, 'A')
+        q_evict(1, 1, 2, 'A')
+        f_mul(0, 1, 0, 5)
+        k_matmul(0, 1, 3)
+        u_matmul(1, 2, 6)
+        u_matmul(1, 1, 1)
+        f_quantize2(0)
+        u_evict(1, 2, 6, 'A')
+        u_matmul(1, 0, 2)
+        u_evict(1, 1, 1, 'A')
+        u_matmul(1, 3, 7)
+        q_quantize2(0)
+        u_evict(1, 0, 2, 'A')
+        u_evict(1, 3, 7, 'A')
+        y_matmul(1, 0, 5)
+        y_matmul(0, 0, 6)
+        f_mul(1, 0, 1, 3)
+        y_cast(1, 0, 5)
+        y_out(1, 0, 5, 'A')
+        q_quantize2(1)
+        k_matmul(0, 3, 2)
+        k_matmul(1, 0, 3)
+        f_mul(1, 1, 3, 0)
+        y_matmul(3, 1, 7)
+        k_matmul(1, 1, 5)
+        f_mul(1, 0, 3, 2)
+        y_out(0, 0, 6, 'A')
+        y_out(3, 1, 7, 'A')
+        f_mul(1, 1, 0, 3)
+        y_matmul(1, 1, 1)
+        f_mul(1, 0, 0, 4)
+        y_matmul(0, 1, 2)
+        f_mul(1, 1, 1, 5)
+        y_cast(0, 0, 6)
+        y_cast(1, 1, 1)
+        k_matmul(0, 2, 7)
+        y_out(0, 1, 2, 'A')
+        f_mul(1, 0, 2, 7)
+        k_matmul(1, 2, 6)
+        y_matmul(2, 0, 3)
+        y_cast(0, 1, 2)
+        f_mul(1, 1, 2, 6)
         f_quantize(1, 0)
-        y_transpose(1, 3)
+        y_matmul(3, 0, 0)
+        y_out(3, 0, 0, 'A')
+        y_transpose(0, 7)
         f_quantize(1, 1)
-        y_transpose(0, 2)
-        y_evict(2, 1, 6, 'A')
-        y_store_h(3, 0)
-        y_store_h(2, 0)
-        y_store_h(1, 1)
-        yt_evict(1, 3, 'V')
-        y_matmul(6, 0, 0)
-        y_matmul(6, 1, 7)
-        y_cast(2, 0, 1)
-        y_evict(6, 0, 0, 'V')
-        y_matmul(4, 1, 4)
-        y_matmul(4, 0, 3)
-        yt_evict(0, 2, 'A')
-        y_quantize(1)
-        y_store_h(0, 0)
-        y_cast(2, 1, 6)
-        y_matmul(7, 1, 6)
-        y_matmul(5, 1, 0)
-        y_evict(6, 1, 7, 'A')
-        y_round(6, 'V')
-        y_store_h(2, 1)
-        y_matmul(5, 0, 1)
-        y_quantize(0)
-        y_evict(7, 1, 6, 'V')
-        y_store_h(6, 0)
-        y_transpose(3, 7)
-        y_evict(4, 1, 4, 'A')
-        y_store_h(3, 1)
-        y_evict(4, 0, 3, 'A')
-        yt_evict(3, 7, 'A')
-        y_evict(5, 1, 0, 'V')
-        y_store_h(6, 1)
-        y_transpose(2, 0)
-        y_evict(5, 0, 1, 'V')
-        words_store(0, 2)
-        y_store_h(4, 1)
-        y_round(5, 'V')
-        y_store_h(4, 0)
+        y_out(1, 1, 1, 'A')
+        y_transpose(1, 5)
+        y_out(2, 0, 3, 'V')
+        y_matmul(2, 1, 6)
+        y_out(2, 1, 6, 'A')
+        y_matmul(7, 1, 0)
+        yt_evict(1, 5, 'V')
+        y_matmul(5, 1, 2)
+        y_round2(1)
+        y_out(7, 1, 0, 'A')
+        y_matmul(4, 0, 4)
+        y_matmul(4, 1, 6)
+        y_matmul(5, 0, 5)
+        yt_evict(0, 7, 'A')
+        y_transpose(3, 3)
+        y_out(5, 1, 2, 'A')
+        y_transpose(2, 7)
+        y_out(4, 0, 4, 'V')
+        y_out(4, 1, 6, 'A')
+        y_out(5, 0, 5, 'A')
+        y_matmul(6, 0, 4)
+        planes2(0)
+        yt_evict(3, 3, 'A')
+        y_round2(2)
+        yt_evict(2, 7, 'A')
+        y_matmul(6, 1, 6)
+        y_out(6, 1, 6, 'A')
         y_matmul(7, 0, 2)
-        yt_evict(2, 0, 'A')
-        y_evict(7, 0, 2, 'A')
-        y_round(4, 'G')
+        yt_matmul(7, 0, 0)
+        planes2(1)
+        y_transpose(5, 3)
+        y_out(6, 0, 4, 'A')
+        y_out(7, 0, 2, 'V')
         y_transpose(4, 6)
-        y_store_h(7, 1)
-        y_quantize(3)
-        yt_evict(4, 6, 'A')
-        y_transpose(5, 4)
-        y_quantize(2)
-        y_round(7, 'V')
-        y_transpose(6, 0)
-        y_quantize(4)
-        yt_evict(6, 0, 'V')
-        yt_evict(5, 4, 'A')
-        y_store_h(5, 0)
-        y_transpose(7, 1)
-        y_quantize(5)
-        y_store_h(5, 1)
         scales_store(0, 4)
-        yt_evict(7, 1, 'A')
-        y_store_h(7, 0)
-        words_store(2, 4)
-        y_quantize(6)
-        words_store(4, 6)
-        y_quantize(7)
-        words_store(6, 8)
+        y_round(6, 'V')
+        yt_matmul(7, 1, 1)
+        yt_round(7, 0, 0, 'A')
+        yt_evict(5, 3, 'A')
+        y_transpose(6, 0)
+        yt_evict(4, 6, 'V')
+        yt_round(7, 1, 1, 'V')
+        planes2(2)
+        yt_evict(6, 0, 'A')
+        planes2(3)
         scales_store(4, 8)

@@ -166,19 +166,19 @@ def tile_cauchytransferfunctionfilter_x2_kernel(
         def cols(half):
             return slice(256 * half, 256 * (half + 1))
 
-        def lorentz4():
+        def lor_sq4():
             for t in range(PACK):
                 nc.scalar.activation(
                     out=dist[:, t, :], in_=om_row[:], func=ACT.Square, bias=nu_col[:, t : t + 1], scale=-1.0
                 )
-            for half in range(2):
-                nc.scalar.activation(
-                    out=dist[:, :, cols(half)], in_=dist[:, :, cols(half)], func=ACT.Abs_reciprocal_sqrt, bias=0.25
-                )
-            for half in range(2):
-                nc.scalar.activation(
-                    out=dist[:, :, cols(half)], in_=dist[:, :, cols(half)], func=ACT.Square
-                )
+
+        def lor_ars(half):
+            nc.scalar.activation(
+                out=dist[:, :, cols(half)], in_=dist[:, :, cols(half)], func=ACT.Abs_reciprocal_sqrt, bias=0.25
+            )
+
+        def lor_sq2(half):
+            nc.scalar.activation(out=dist[:, :, cols(half)], in_=dist[:, :, cols(half)], func=ACT.Square)
 
         def de_times_b():
             nc.gpsimd.tensor_scalar(
@@ -410,164 +410,177 @@ def tile_cauchytransferfunctionfilter_x2_kernel(
         setup()
         load_col('om')
         load_p_words()
-        load_col('nu')
-        load_x(0)
-        permute_p_words()
-        x_interleave(0, 'V')
         spread_om()
-        load_col('b')
+        load_col('nu')
         load_x(1)
-        x_interleave(1, 'V')
+        load_x(0)
+        lor_sq4()
+        lor_ars(1)
         load_p_scales()
-        permute_p_scales()
-        x_quantize2(0)
-        load_q(2)
-        lorentz4()
-        q_transpose(2, 0, 5)
-        load_c()
-        de_times_b()
-        q_transpose(2, 1, 2)
-        g_real(0)
-        load_x(2)
-        u_matmul(0, 3, 1)
-        q_evict(2, 0, 5, 'A')
-        g_real(1)
-        u_evict(0, 3, 1, 'A')
-        u_matmul(0, 1, 4)
+        permute_p_words()
+        load_col('b')
         load_q(0)
-        u_matmul(0, 2, 6)
-        g_imag(1)
-        u_evict(0, 2, 6, 'A')
-        q_evict(2, 1, 2, 'A')
+        x_interleave(1, 'V')
+        load_x(2)
+        x_interleave(0, 'V')
+        lor_ars(0)
+        lor_sq2(1)
+        permute_p_scales()
         q_transpose(0, 0, 3)
-        u_matmul(0, 0, 7)
-        load_q(1)
-        g_quantize(0)
-        q_transpose(1, 0, 6)
-        u_evict(0, 1, 4, 'A')
+        x_quantize2(0)
+        q_transpose(0, 1, 6)
+        u_matmul(0, 1, 0)
         q_evict(0, 0, 3, 'A')
-        load_x(3)
-        k_matmul(0, 0, 1)
-        k_matmul(0, 2, 3)
-        u_evict(0, 0, 7, 'A')
-        x_interleave(2, 'A')
-        g_imag(0)
-        f_mul(0, 0, 0, 1)
-        x_interleave(3, 'A')
-        k_matmul(0, 1, 5)
-        g_quantize(1)
-        f_mul(0, 0, 2, 3)
-        k_matmul(1, 2, 2)
-        k_matmul(0, 3, 1)
+        load_c()
+        u_matmul(0, 3, 7)
+        lor_sq2(0)
+        de_times_b()
+        u_matmul(0, 2, 5)
         load_q(3)
-        k_matmul(1, 1, 4)
-        f_mul(0, 0, 1, 5)
-        k_matmul(1, 3, 7)
-        f_mul(0, 1, 2, 2)
-        f_mul(0, 0, 3, 1)
-        f_mul(0, 1, 3, 7)
-        q_evict(1, 0, 6, 'A')
-        k_matmul(1, 0, 5)
-        f_mul(0, 1, 1, 4)
+        g_imag(1)
+        u_evict(0, 3, 7, 'A')
+        load_q(1)
+        u_matmul(0, 0, 3)
+        q_evict(0, 1, 6, 'A')
+        q_transpose(1, 1, 4)
+        g_imag(0)
+        u_evict(0, 0, 3, 'A')
+        u_evict(0, 1, 0, 'A')
+        g_real(0)
+        g_quantize(1)
         q_transpose(3, 0, 3)
-        q_transpose(1, 1, 2)
-        q_transpose(0, 1, 1)
-        q_transpose(3, 1, 7)
-        k_matmul(0, 0, 4)
+        k_matmul(1, 1, 0)
+        k_matmul(1, 3, 1)
+        k_matmul(1, 0, 2)
+        g_real(1)
+        load_x(3)
+        f_mul(0, 1, 1, 0)
+        g_quantize(0)
+        u_evict(0, 2, 5, 'A')
+        q_transpose(3, 1, 0)
+        x_interleave(2, 'A')
+        f_mul(0, 1, 0, 2)
+        f_mul(0, 1, 3, 1)
+        k_matmul(0, 0, 5)
+        x_interleave(3, 'A')
+        k_matmul(0, 0, 7)
         q_evict(3, 0, 3, 'A')
-        x_quantize2(1)
-        q_evict(3, 1, 7, 'A')
-        k_matmul(1, 3, 0)
-        q_evict(0, 1, 1, 'A')
-        q_evict(1, 1, 2, 'A')
-        f_mul(0, 1, 0, 5)
-        k_matmul(0, 1, 3)
-        u_matmul(1, 2, 6)
-        u_matmul(1, 1, 1)
-        f_quantize2(0)
-        u_evict(1, 2, 6, 'A')
-        u_matmul(1, 0, 2)
-        u_evict(1, 1, 1, 'A')
-        u_matmul(1, 3, 7)
-        q_quantize2(0)
-        u_evict(1, 0, 2, 'A')
-        u_evict(1, 3, 7, 'A')
-        y_matmul(1, 0, 5)
-        y_matmul(0, 0, 6)
-        f_mul(1, 0, 1, 3)
-        y_cast(1, 0, 5)
-        y_out(1, 0, 5, 'A')
-        q_quantize2(1)
-        k_matmul(0, 3, 2)
-        k_matmul(1, 0, 3)
-        f_mul(1, 1, 3, 0)
-        y_matmul(3, 1, 7)
-        k_matmul(1, 1, 5)
-        f_mul(1, 0, 3, 2)
-        y_out(0, 0, 6, 'A')
-        y_out(3, 1, 7, 'A')
-        f_mul(1, 1, 0, 3)
-        y_matmul(1, 1, 1)
-        f_mul(1, 0, 0, 4)
-        y_matmul(0, 1, 2)
-        f_mul(1, 1, 1, 5)
-        y_cast(0, 0, 6)
-        y_cast(1, 1, 1)
-        k_matmul(0, 2, 7)
-        y_out(0, 1, 2, 'A')
-        f_mul(1, 0, 2, 7)
+        k_matmul(0, 2, 6)
+        load_q(2)
+        k_matmul(0, 1, 2)
+        q_transpose(2, 0, 1)
+        q_evict(3, 1, 0, 'A')
+        f_mul(0, 0, 0, 7)
+        f_mul(0, 0, 1, 2)
+        f_mul(0, 0, 2, 6)
+        q_transpose(2, 1, 7)
+        q_transpose(1, 0, 2)
+        q_evict(2, 1, 7, 'A')
+        k_matmul(0, 3, 3)
+        q_evict(2, 0, 1, 'A')
+        q_evict(1, 0, 2, 'A')
         k_matmul(1, 2, 6)
-        y_matmul(2, 0, 3)
-        y_cast(0, 1, 2)
+        k_matmul(0, 3, 0)
+        x_quantize2(1)
+        f_mul(0, 0, 3, 3)
+        f_mul(0, 1, 2, 6)
+        u_matmul(1, 1, 7)
+        u_evict(1, 1, 7, 'A')
+        q_quantize2(1)
+        q_evict(1, 1, 4, 'A')
+        u_matmul(1, 2, 1)
+        u_matmul(1, 0, 2)
+        f_quantize2(0)
+        u_evict(1, 0, 2, 'A')
+        q_quantize2(0)
+        u_matmul(1, 3, 7)
+        f_mul(1, 0, 0, 5)
+        k_matmul(1, 2, 6)
+        u_evict(1, 3, 7, 'A')
+        k_matmul(0, 2, 2)
+        y_matmul(3, 1, 4)
+        u_evict(1, 2, 1, 'A')
+        y_out(3, 1, 4, 'A')
+        y_matmul(2, 0, 7)
+        y_out(2, 0, 7, 'A')
+        y_matmul(0, 0, 3)
+        y_cast(0, 0, 3)
+        y_matmul(0, 1, 4)
+        y_cast(0, 1, 4)
+        k_matmul(0, 1, 1)
+        y_out(0, 1, 4, 'A')
+        f_mul(1, 0, 3, 0)
         f_mul(1, 1, 2, 6)
+        y_matmul(1, 1, 5)
+        f_mul(1, 0, 2, 2)
+        y_out(0, 0, 3, 'A')
+        k_matmul(1, 3, 7)
+        k_matmul(1, 0, 0)
+        f_mul(1, 0, 1, 1)
+        k_matmul(1, 1, 6)
+        f_mul(1, 1, 0, 0)
+        y_out(1, 1, 5, 'A')
+        y_matmul(2, 1, 1)
+        y_matmul(1, 0, 2)
         f_quantize(1, 0)
-        y_matmul(3, 0, 0)
-        y_out(3, 0, 0, 'A')
-        y_transpose(0, 7)
+        y_out(2, 1, 1, 'A')
+        y_matmul(3, 0, 3)
+        y_pass(5, 0, 0, 0)
+        y_cast(1, 1, 5)
+        f_mul(1, 1, 1, 6)
+        y_out(3, 0, 3, 'A')
+        y_pass(6, 0, 1, 0)
+        f_mul(1, 1, 3, 7)
         f_quantize(1, 1)
-        y_out(1, 1, 1, 'A')
-        y_transpose(1, 5)
-        y_out(2, 0, 3, 'V')
-        y_matmul(2, 1, 6)
-        y_out(2, 1, 6, 'A')
-        y_matmul(7, 1, 0)
-        yt_evict(1, 5, 'V')
-        y_matmul(5, 1, 2)
+        y_pass(7, 0, 4, 0)
+        y_pass(4, 0, 6, 0)
         y_round2(1)
-        y_out(7, 1, 0, 'A')
-        y_matmul(4, 0, 4)
-        y_matmul(4, 1, 6)
-        y_matmul(5, 0, 5)
-        yt_evict(0, 7, 'A')
+        y_pass(5, 1, 5, 0)
+        y_pass(4, 1, 3, 0)
+        y_out(1, 0, 2, 'A')
+        y_pass(5, 1, 5, 1)
+        y_pass(5, 0, 0, 1)
+        y_cast(1, 0, 2)
+        y_pass(6, 0, 1, 1)
+        y_pass(4, 1, 3, 1)
+        y_pass(4, 0, 6, 1)
+        y_out(5, 1, 5, 'A')
+        y_out(5, 0, 0, 'V')
+        y_pass(6, 1, 2, 0)
+        y_out(6, 0, 1, 'A')
+        y_out(4, 1, 3, 'V')
+        y_pass(6, 1, 2, 1)
+        y_pass(7, 0, 4, 1)
+        y_out(4, 0, 6, 'A')
+        y_out(7, 0, 4, 'V')
+        y_transpose(0, 7)
+        y_transpose(1, 5)
         y_transpose(3, 3)
-        y_out(5, 1, 2, 'A')
-        y_transpose(2, 7)
-        y_out(4, 0, 4, 'V')
-        y_out(4, 1, 6, 'A')
-        y_out(5, 0, 5, 'A')
-        y_matmul(6, 0, 4)
-        planes2(0)
-        yt_evict(3, 3, 'A')
+        y_out(6, 1, 2, 'A')
+        y_pass(7, 1, 0, 0)
+        yt_evict(0, 7, 'A')
+        y_pass(7, 1, 0, 1)
         y_round2(2)
-        yt_evict(2, 7, 'A')
-        y_matmul(6, 1, 6)
-        y_out(6, 1, 6, 'A')
-        y_matmul(7, 0, 2)
-        yt_matmul(7, 0, 0)
-        planes2(1)
-        y_transpose(5, 3)
-        y_out(6, 0, 4, 'A')
-        y_out(7, 0, 2, 'V')
-        y_transpose(4, 6)
-        scales_store(0, 4)
+        y_transpose(2, 1)
+        yt_evict(1, 5, 'A')
+        y_transpose(4, 7)
+        yt_evict(3, 3, 'A')
+        planes2(0)
         y_round(6, 'V')
-        yt_matmul(7, 1, 1)
-        yt_round(7, 0, 0, 'A')
-        yt_evict(5, 3, 'A')
-        y_transpose(6, 0)
-        yt_evict(4, 6, 'V')
-        yt_round(7, 1, 1, 'V')
+        yt_evict(2, 1, 'A')
+        y_out(7, 1, 0, 'A')
+        y_transpose(5, 2)
+        planes2(1)
+        yt_evict(4, 7, 'A')
+        yt_matmul(7, 1, 3)
+        yt_evict(5, 2, 'V')
+        y_transpose(6, 6)
+        yt_round(7, 1, 3, 'A')
+        scales_store(0, 4)
+        yt_evict(6, 6, 'A')
         planes2(2)
-        yt_evict(6, 0, 'A')
-        planes2(3)
+        yt_matmul(7, 0, 5)
+        yt_round(7, 0, 5, 'A')
+        planes1(6)
+        planes1(7)
         scales_store(4, 8)

@@ -18,7 +18,10 @@ ACT = mybir.ActivationFunctionType
 
 P = 128
 PACK = 4
-W = 512
+PASS = P * PACK
+PAIR = 2 * P
+RUN = 4
+YT_BUFS = 4
 
 
 def tile_cauchytransferfunctionfilter_x2_kernel(
@@ -36,17 +39,17 @@ def tile_cauchytransferfunctionfilter_x2_kernel(
         def tiles(name, count, shape, dtype):
             return [tile("%s%d" % (name, i), shape, dtype) for i in range(count)]
 
-        bank = [ps.tile([P, W], F32, name="bank%d" % i) for i in range(8)]
+        bank = [ps.tile([P, PASS], F32, name="bank%d" % i) for i in range(8)]
 
         ident_bf = tile("ident_bf", [P, P], BF16)
         ident_f32 = tile("ident_f32", [P, P], F32)
-        warm_in = tile("warm_in", [P, 1], F32)
-        warm_out = tile("warm_out", [P, 1], F32)
+        table_in = tile("table_in", [P, 1], F32)
+        table_out = tile("table_out", [P, 1], F32)
         om_col = tile("om_col", [P, PACK], BF16)
         nu_col = tile("nu_col", [P, PACK], BF16)
         b_col = tile("b_col", [P, PACK], BF16)
         om_row = tile("om_row", [P, M], BF16)
-        dist = tile("dist", [P, PACK, M], F32)
+        lorentz = tile("lorentz", [P, PACK, M], F32)
         half_b = tile("half_b", [P, PACK], F32)
         de_b = tile("de_b", [P, PACK, M], F32)
         g_bf = tiles("g_bf", 2, [P, M, PACK], BF16)
@@ -63,16 +66,16 @@ def tile_cauchytransferfunctionfilter_x2_kernel(
         x_codes = tile("x_codes", [P, 4, D], U32)
         x_scale = tile("x_scale", [P, 4, D], U8)
         q_raw = tiles("q_raw", 4, [P, 2, 2 * M], BF16)
-        q_bf = tile("q_bf", [P, 4, 2, 2 * W], BF16)
-        q_codes = tile("q_codes", [P, 4, W], U32)
-        q_scale = tile("q_scale", [P, 4, W], U8)
-        u_sb = tiles("u_sb", 2, [P, 4, W], F32)
+        q_bf = tile("q_bf", [P, 4, 2, 2 * PASS], BF16)
+        q_codes = tile("q_codes", [P, 4, PASS], U32)
+        q_scale = tile("q_scale", [P, 4, PASS], U8)
+        u_sb = tiles("u_sb", 2, [P, PACK, PASS], F32)
         f_bf = tile("f_bf", [P, 2, PACK * D], BF16)
         f_codes = tile("f_codes", [P, 4, D], U32)
         f_scale = tile("f_scale", [P, 4, D], U8)
         y32 = tile("y32", [P, 8, 2, D], F32)
         y_bf = tile("y_bf", [P, 4, 2 * D], BF16)
-        yt_bf = tile("yt_bf", [P, 4, 2 * D], BF16)
+        yt_bf = tile("yt_bf", [P, YT_BUFS, 2 * D], BF16)
         y_codes = tile("y_codes", [P, B * S], U32)
         y_scale = tile("y_scale", [P, B * S], U8)
 
@@ -80,107 +83,104 @@ def tile_cauchytransferfunctionfilter_x2_kernel(
         y_rounded = [q_bf[:, 0], q_bf[:, 1], y_bf[:, 0:2, :], y_bf[:, 2:4, :]]
         y_words = {}
 
-        def copy_on(eng, dst, src):
-            if eng == "V":
+        def copy_on(engine, dst, src):
+            if engine == "vector":
                 nc.vector.tensor_copy(out=dst, in_=src)
-            elif eng == "A":
-                nc.scalar.copy(out=dst, in_=src)
             else:
-                nc.gpsimd.tensor_scalar(out=dst, in0=src, scalar1=1.0, scalar2=1.0, op0=ALU.mult, op1=ALU.mult)
+                nc.scalar.copy(out=dst, in_=src)
 
-        def load_col(name):
-            dst, vec = {"om": (om_col, om), "nu": (nu_col, nu), "b": (b_col, b)}[name]
+        def flat(ap):
+            return ap.rearrange("p a b -> p (a b)")
+
+        def cols(width, i):
+            return slice(width * i, width * (i + 1))
+
+        def quantize(codes, scale, src):
+            nc.vector.quantize_mx(out=codes.bitcast(FP8X4), scales=scale, in_=src)
+
+        def setup():
+            nc.vector.memset(table_in[:], 1.0)
+            nc.vector.memset(flat(psc_raw[:]).bitcast(I32), 0)
+            nc.vector.memset(csc[:].bitcast(I32), 0)
+            nc.scalar.activation(out=table_out[:], in_=table_in[:], func=ACT.Abs_reciprocal_sqrt)
+            make_identity(nc, ident_bf[:])
+            make_identity(nc, ident_f32[:])
+
+        def load_col(dst, vec):
             nc.sync.dma_start(out=dst[:], in_=vec.rearrange("(p t) -> p t", t=PACK))
 
         def load_x(i):
             bi, g = divmod(i, 2)
             nc.sync.dma_start(
-                out=x_raw[:, i, :], in_=x[bi, W * g : W * (g + 1), :].rearrange("(p j) d -> p (j d)", j=PACK)
+                out=x_raw[:, i, :], in_=x[bi, cols(PASS, g), :].rearrange("(p t) d -> p (t d)", t=PACK)
             )
 
         def load_q(i):
-            half, ci = divmod(i, 2)
+            half, part = divmod(i, 2)
             nc.sync.dma_start(
                 out=q_raw[i][:],
-                in_=q[ci, W * half : W * (half + 1), :].rearrange("(a p h) m -> p a (h m)", a=2, h=2),
+                in_=q[part, cols(PASS, half), :].rearrange("(a p h) m -> p a (h m)", a=2, h=2),
             )
 
         def load_p_words():
             nc.sync.dma_start(out=pw_raw[:].bitcast(I32), in_=p_words.rearrange("g p n -> p g n").bitcast(I32))
 
         def load_p_scales():
-            for quad in range(4):
+            for quad in range(PACK):
                 nc.sync.dma_start(
                     out=psc_raw[32 * quad : 32 * quad + 4, :, :].bitcast(I32),
-                    in_=p_scales[:, 4 * quad : 4 * quad + 4, :].rearrange("g r n -> r g n").bitcast(I32),
+                    in_=p_scales[:, cols(4, quad), :].rearrange("g r n -> r g n").bitcast(I32),
                 )
 
         def load_c():
             nc.sync.dma_start(out=cw[:].bitcast(I32), in_=c_words[0].bitcast(I32))
-            for quad in range(4):
+            for quad in range(PACK):
                 nc.sync.dma_start(
                     out=csc[32 * quad : 32 * quad + 4, :].bitcast(I32),
-                    in_=c_scales[0, 4 * quad : 4 * quad + 4, :].bitcast(I32),
+                    in_=c_scales[0, cols(4, quad), :].bitcast(I32),
                 )
-
-        def quantize(codes, scale, src):
-            nc.vector.quantize_mx(out=codes.bitcast(FP8X4), scales=scale, in_=src)
-
-        def flat(ap):
-            return ap.rearrange("p a b -> p (a b)")
 
         def permute_p_words():
             nc.vector.tensor_copy(
-                out=pw[:].rearrange("p t g (m e) -> p t (g m) e", e=2),
-                in_=pw_raw[:].rearrange("p g (m t e) -> p t (g m) e", t=PACK, e=2),
+                out=pw[:].rearrange("p t g (w e) -> p t (g w) e", e=2),
+                in_=pw_raw[:].rearrange("p g (w t e) -> p t (g w) e", t=PACK, e=2),
             )
 
         def permute_p_scales():
             nc.vector.tensor_copy(
-                out=psc[:].rearrange("p t g m -> p t (g m)"),
-                in_=psc_raw[:].rearrange("p g (m t) -> p t (g m)", t=PACK),
+                out=psc[:].rearrange("p t g w -> p t (g w)"),
+                in_=psc_raw[:].rearrange("p g (w t) -> p t (g w)", t=PACK),
             )
 
-        def x_interleave(i, eng="V"):
+        def x_interleave(i, engine):
             copy_on(
-                eng,
-                x_grouped[i // 2][:, i % 2, :].rearrange("p (c i t) -> p c t i", i=4, t=4),
-                x_raw[:, i, :].rearrange("p (t c i) -> p c t i", i=4, t=4),
+                engine,
+                x_grouped[i // 2][:, i % 2, :].rearrange("p (c r t) -> p c t r", r=RUN, t=PACK),
+                x_raw[:, i, :].rearrange("p (t c r) -> p c t r", r=RUN, t=PACK),
             )
 
-        def x_quantize(i):
-            quantize(x_codes[:, i, :], x_scale[:, i, :], x_grouped[i // 2][:, i % 2, :])
-
-        def x_quantize2(bi):
-            sl = slice(2 * bi, 2 * bi + 2)
+        def x_quantize(bi):
+            sl = cols(2, bi)
             quantize(flat(x_codes[:, sl, :]), flat(x_scale[:, sl, :]), flat(x_grouped[bi]))
 
-        def spread_om():
-            view = bank[0][:].bitcast(BF16)
+        def spread_om(bk):
+            view = bank[bk][:].bitcast(BF16)
             for t in range(PACK):
-                nc.tensor.transpose(
-                    view[:, P * t : P * (t + 1)], om_col[:, t : t + 1].to_broadcast([P, P]), ident_bf[:]
-                )
+                nc.tensor.transpose(view[:, cols(P, t)], om_col[:, t : t + 1].to_broadcast([P, P]), ident_bf[:])
             nc.scalar.copy(out=om_row[:], in_=view[:, 0:M])
 
-        def cols(half):
-            return slice(256 * half, 256 * (half + 1))
-
-        def lor_sq4():
+        def make_lorentz():
             for t in range(PACK):
                 nc.scalar.activation(
-                    out=dist[:, t, :], in_=om_row[:], func=ACT.Square, bias=nu_col[:, t : t + 1], scale=-1.0
+                    out=lorentz[:, t, :], in_=om_row[:], func=ACT.Square, bias=nu_col[:, t : t + 1], scale=-1.0
                 )
+            halves = [lorentz[:, :, cols(M // 2, half)] for half in range(2)]
+            for ap in halves:
+                nc.scalar.activation(out=ap, in_=ap, func=ACT.Abs_reciprocal_sqrt, bias=0.25)
+            for ap in halves:
+                nc.scalar.activation(out=ap, in_=ap, func=ACT.Square)
 
-        def lor_ars(half):
-            nc.scalar.activation(
-                out=dist[:, :, cols(half)], in_=dist[:, :, cols(half)], func=ACT.Abs_reciprocal_sqrt, bias=0.25
-            )
-
-        def lor_sq2(half):
-            nc.scalar.activation(out=dist[:, :, cols(half)], in_=dist[:, :, cols(half)], func=ACT.Square)
-
-        def de_times_b():
+        def make_factors():
             nc.gpsimd.tensor_scalar(
                 out=half_b[:], in0=b_col[:], scalar1=0.5, scalar2=1.0, op0=ALU.mult, op1=ALU.mult
             )
@@ -190,20 +190,16 @@ def tile_cauchytransferfunctionfilter_x2_kernel(
                     op0=ALU.subtract, op1=ALU.mult,
                 )
 
-        def by_run(ap):
-            return ap.rearrange("p t (c i) -> p c t i", i=4)
-
-        def g_product(part, half, factor):
+        def g_product(part, half):
+            sl = cols(M // 2, half)
+            if part == 0:
+                factor = half_b[:].unsqueeze(1).unsqueeze(3).to_broadcast([P, M // 2 // RUN, PACK, RUN])
+            else:
+                factor = de_b[:, :, sl].rearrange("p t (c r) -> p c t r", r=RUN)
             nc.vector.tensor_tensor(
-                out=g_bf[part][:, cols(half), :].rearrange("p (c i) t -> p c t i", i=4),
-                in0=by_run(dist[:, :, cols(half)]), in1=factor, op=ALU.mult,
+                out=g_bf[part][:, sl, :].rearrange("p (c r) t -> p c t r", r=RUN),
+                in0=lorentz[:, :, sl].rearrange("p t (c r) -> p c t r", r=RUN), in1=factor, op=ALU.mult,
             )
-
-        def g_real(half):
-            g_product(0, half, half_b[:].unsqueeze(1).unsqueeze(3).to_broadcast([P, 64, PACK, 4]))
-
-        def g_imag(half):
-            g_product(1, half, by_run(de_b[:, :, cols(half)]))
 
         def g_quantize(part):
             quantize(g_codes[part][:], g_scale[part][:], flat(g_bf[part][:]))
@@ -213,22 +209,17 @@ def tile_cauchytransferfunctionfilter_x2_kernel(
             for h in range(2):
                 for u in range(2):
                     nc.tensor.transpose(
-                        bank[bk][:, P * (2 * h + u) : P * (2 * h + u + 1)],
-                        words[:, 256 * h + u : 256 * (h + 1) : 2], ident_f32[:],
+                        bank[bk][:, cols(P, 2 * h + u)], words[:, PAIR * h + u : PAIR * (h + 1) : 2], ident_f32[:]
                     )
 
-        def q_evict(i, a, bk, eng="A"):
-            copy_on(
-                eng,
-                q_bf[:, i, a, :].bitcast(F32).rearrange("p (s r) -> p s r", r=4),
-                bank[bk][:].rearrange("p (r s) -> p s r", r=4),
+        def q_evict(i, a, bk):
+            nc.scalar.copy(
+                out=q_bf[:, i, a, :].bitcast(F32).rearrange("p (s r) -> p s r", r=4),
+                in_=bank[bk][:].rearrange("p (r s) -> p s r", r=4),
             )
 
-        def q_quantize(i):
-            quantize(q_codes[:, i, :], q_scale[:, i, :], flat(q_bf[:, i]))
-
-        def q_quantize2(half):
-            sl = slice(2 * half, 2 * half + 2)
+        def q_quantize(half):
+            sl = cols(2, half)
             quantize(
                 flat(q_codes[:, sl, :]), flat(q_scale[:, sl, :]), q_bf[:, sl].rearrange("p c a w -> p (c a w)")
             )
@@ -237,350 +228,254 @@ def tile_cauchytransferfunctionfilter_x2_kernel(
             for t in range(PACK):
                 for g in range(2):
                     nc.tensor.matmul_mx(
-                        out=bank[bk][:, P * t : P * (t + 1)],
+                        out=bank[bk][:, cols(P, t)],
                         lhsT=pw[:, t, g, :].bitcast(FP4X4), lhsT_scale=psc[:, t, g, :],
-                        rhs=x_codes[:, 2 * bi + g, P * j : P * (j + 1)].bitcast(FP8X4),
-                        rhs_scale=x_scale[:, 2 * bi + g, P * j : P * (j + 1)],
+                        rhs=x_codes[:, 2 * bi + g, cols(P, j)].bitcast(FP8X4),
+                        rhs_scale=x_scale[:, 2 * bi + g, cols(P, j)],
                         start=(g == 0), stop=(g == 1),
                     )
 
         def k_matmul(part, j, bk):
             for t in range(PACK):
                 nc.tensor.matmul_mx(
-                    out=bank[bk][:, P * t : P * (t + 1)],
-                    lhsT=g_codes[part][:, P * t : P * (t + 1)].bitcast(FP8X4),
-                    lhsT_scale=g_scale[part][:, P * t : P * (t + 1)],
-                    rhs=cw[:, 2 * P * j : 2 * P * (j + 1)].bitcast(FP4X4),
-                    rhs_scale=csc[:, P * j : P * (j + 1)],
+                    out=bank[bk][:, cols(P, t)],
+                    lhsT=g_codes[part][:, cols(P, t)].bitcast(FP8X4), lhsT_scale=g_scale[part][:, cols(P, t)],
+                    rhs=cw[:, cols(2 * P, j)].bitcast(FP4X4), rhs_scale=csc[:, cols(P, j)],
                     start=True, stop=True,
                 )
 
-        def by_slot(bk):
-            return bank[bk][:].rearrange("p (t a e) -> p e a t", t=4, e=4)
+        def in_f_order(bk):
+            return bank[bk][:].rearrange("p (t a e) -> p e a t", t=PACK, e=PACK)
 
-        def u_evict(bi, j, bk, eng="A"):
-            copy_on(eng, u_sb[bi][:, j, :].rearrange("p (e a t) -> p e a t", e=4, t=4), by_slot(bk))
+        def u_chunk(bi, j):
+            return u_sb[bi][:, j, :].rearrange("p (e a t) -> p e a t", e=PACK, t=PACK)
 
-        def f_mul(bi, part, j, bk):
+        def u_evict(bi, j, bk):
+            nc.scalar.copy(out=u_chunk(bi, j), in_=in_f_order(bk))
+
+        def f_product(bi, part, j, bk):
             nc.vector.tensor_tensor(
-                out=f_bf[:, part, :].rearrange("p (e w t) -> p e w t", e=4, t=4)[:, :, 32 * j : 32 * (j + 1), :],
-                in0=by_slot(bk),
-                in1=u_sb[bi][:, j, :].rearrange("p (e a t) -> p e a t", e=4, t=4), op=ALU.mult,
+                out=f_bf[:, part, :].rearrange("p (e w t) -> p e w t", e=PACK, t=PACK)[:, :, cols(P // PACK, j), :],
+                in0=in_f_order(bk), in1=u_chunk(bi, j), op=ALU.mult,
             )
 
-        def f_quantize(bi, part):
-            quantize(f_codes[:, 2 * bi + part, :], f_scale[:, 2 * bi + part, :], f_bf[:, part, :])
+        def f_quantize(bi, first, count):
+            sl = slice(2 * bi + first, 2 * bi + first + count)
+            quantize(flat(f_codes[:, sl, :]), flat(f_scale[:, sl, :]), flat(f_bf[:, first : first + count, :]))
 
-        def f_quantize2(bi):
-            sl = slice(2 * bi, 2 * bi + 2)
-            quantize(flat(f_codes[:, sl, :]), flat(f_scale[:, sl, :]), flat(f_bf[:]))
+        def tile_operands(n, part):
+            bi, rows = divmod(n, S // P)
+            half, place = divmod(rows, PASS // P)
+            i = 2 * half + part
+            return q_codes[:, i, cols(P, place)].bitcast(FP8X4), q_scale[:, i, cols(P, place)], 2 * bi + part
 
-        def y_pass(pair, h, bk, part):
-            bi, blk = divmod(pair, 4)
-            half, a = divmod(blk, 2)
-            sl = slice(256 * a + P * h, 256 * a + P * (h + 1))
-            nc.tensor.matmul_mx(
-                out=bank[bk][:],
-                lhsT=q_codes[:, 2 * half + part, sl].bitcast(FP8X4), lhsT_scale=q_scale[:, 2 * half + part, sl],
-                rhs=f_codes[:, 2 * bi + part, :].bitcast(FP8X4), rhs_scale=f_scale[:, 2 * bi + part, :],
-                start=(part == 0), stop=(part == 1),
-            )
-
-        def y_matmul(pair, h, bk):
-            y_pass(pair, h, bk, 0)
-            y_pass(pair, h, bk, 1)
-
-        def y_evict(pair, h, bk, eng="A"):
+        def y_tile(n, bk, engine):
+            for part in range(2):
+                codes, scale, fi = tile_operands(n, part)
+                nc.tensor.matmul_mx(
+                    out=bank[bk][:], lhsT=codes, lhsT_scale=scale,
+                    rhs=f_codes[:, fi, :].bitcast(FP8X4), rhs_scale=f_scale[:, fi, :],
+                    start=(part == 0), stop=(part == 1),
+                )
+            dst = y32[:, n // 2, n % 2, :]
             copy_on(
-                eng,
-                y32[:, pair, h, :].rearrange("p (w e) -> p w e", e=4),
-                bank[bk][:].rearrange("p (e w) -> p w e", e=4),
+                engine, dst.rearrange("p (w e) -> p w e", e=PACK), bank[bk][:].rearrange("p (e w) -> p w e", e=PACK)
             )
+            bi, rows = divmod(n, S // P)
+            nc.sync.dma_start(out=out_0[bi, cols(P, rows), :], in_=dst)
 
-        def yt_matmul(pair, h, bk):
-            bi, blk = divmod(pair, 4)
-            half, a = divmod(blk, 2)
-            sl = slice(256 * a + P * h, 256 * a + P * (h + 1))
-            for t in range(PACK):
-                ch = slice(P * t, P * (t + 1))
-                for part in range(2):
-                    nc.tensor.matmul_mx(
-                        out=bank[bk][:, ch],
-                        lhsT=f_codes[:, 2 * bi + part, ch].bitcast(FP8X4), lhsT_scale=f_scale[:, 2 * bi + part, ch],
-                        rhs=q_codes[:, 2 * half + part, sl].bitcast(FP8X4), rhs_scale=q_scale[:, 2 * half + part, sl],
-                        start=(part == 0), stop=(part == 1),
-                    )
+        def as_words(ap):
+            return ap.bitcast(F32).rearrange("p (u w) -> p u w", u=2)
 
-        def yt_round(pair, h, bk, eng="A"):
-            copy_on(
-                eng,
-                yt_bf[:, pair % 4, W * h : W * (h + 1)].rearrange("p (s t) -> p s t", t=4),
-                bank[bk][:].rearrange("p (t s) -> p s t", t=4),
-            )
-
-        def y_store_h(pair, h):
-            bi, blk = divmod(pair, 4)
-            lo = 256 * blk + P * h
-            nc.sync.dma_start(out=out_0[bi, lo : lo + P, :], in_=y32[:, pair, h, :])
-
-        def y_round(pair, eng="V"):
+        def y_round_from_bank(n, bk):
+            pair, h = divmod(n, 2)
             dst = y_rounded[pair // 2][:, pair % 2, :]
-            copy_on(
-                eng,
-                dst.rearrange("p (u w e) -> p u w e", u=2, e=2),
-                flat(y32[:, pair]).rearrange("p (w u e) -> p u w e", u=2, e=2),
+            nc.scalar.copy(
+                out=dst.rearrange("p (u h w e) -> p h u w e", u=2, h=2, e=2)[:, h],
+                in_=bank[bk][:].rearrange("p (u e w) -> p u w e", u=2, e=2),
             )
-            y_words[pair] = dst.bitcast(F32).rearrange("p (u w) -> p u w", u=2)
+            y_words[pair] = as_words(dst)
 
-        def y_round2(k):
-            dst = flat(y_rounded[k])
+        def y_round_pair(pair):
+            dst = y_rounded[pair // 2][:, pair % 2, :]
             nc.vector.tensor_copy(
                 out=dst.rearrange("p (u w e) -> p u w e", u=2, e=2),
-                in_=y32[:, 2 * k : 2 * k + 2].rearrange("p a h (w u e) -> p u (a h w) e", u=2, e=2),
+                in_=flat(y32[:, pair]).rearrange("p (w u e) -> p u w e", u=2, e=2),
+            )
+            y_words[pair] = as_words(dst)
+
+        def y_round_two_pairs(first):
+            dst = flat(y_rounded[first // 2])
+            nc.vector.tensor_copy(
+                out=dst.rearrange("p (u w e) -> p u w e", u=2, e=2),
+                in_=y32[:, first : first + 2].rearrange("p a h (w u e) -> p u (a h w) e", u=2, e=2),
             )
             for a in range(2):
-                y_words[2 * k + a] = dst.bitcast(F32).rearrange("p (u w) -> p u w", u=2)[:, :, 256 * a : 256 * (a + 1)]
-
-        def y_cast(pair, h, bk, eng="A"):
-            dst = y_rounded[pair // 2][:, pair % 2, :]
-            copy_on(
-                eng,
-                dst.rearrange("p (u h w e) -> p h u w e", u=2, h=2, e=2)[:, h],
-                bank[bk][:].rearrange("p (u e w) -> p u w e", u=2, e=2),
-            )
-            y_words[pair] = dst.bitcast(F32).rearrange("p (u w) -> p u w", u=2)
+                y_words[first + a] = as_words(dst)[:, :, cols(PAIR, a)]
 
         def y_transpose(pair, bk):
             for u in range(2):
                 for h in range(2):
                     nc.tensor.transpose(
-                        bank[bk][:, P * (2 * u + h) : P * (2 * u + h + 1)],
-                        y_words[pair][:, u, P * h : P * (h + 1)], ident_f32[:],
+                        bank[bk][:, cols(P, 2 * u + h)], y_words[pair][:, u, cols(P, h)], ident_f32[:]
                     )
 
-        def yt_evict(pair, bk, eng="A"):
+        def yt_evict(pair, bk, engine):
             copy_on(
-                eng,
-                yt_bf[:, pair % 4, :].bitcast(F32).rearrange("p (w u) -> p w u", u=2),
-                bank[bk][:].rearrange("p (u w) -> p w u", u=2),
+                engine,
+                yt_bf[:, pair % YT_BUFS, :].bitcast(F32).rearrange("p (s u) -> p s u", u=2),
+                bank[bk][:].rearrange("p (u s) -> p s u", u=2),
             )
 
-        def y_quantize(pair):
-            sl = slice(256 * pair, 256 * (pair + 1))
-            quantize(y_codes[:, sl], y_scale[:, sl], yt_bf[:, pair % 4, :])
+        def yt_tile(n, bk):
+            for t in range(PACK):
+                for part in range(2):
+                    codes, scale, fi = tile_operands(n, part)
+                    nc.tensor.matmul_mx(
+                        out=bank[bk][:, cols(P, t)],
+                        lhsT=f_codes[:, fi, cols(P, t)].bitcast(FP8X4), lhsT_scale=f_scale[:, fi, cols(P, t)],
+                        rhs=codes, rhs_scale=scale, start=(part == 0), stop=(part == 1),
+                    )
+            nc.scalar.copy(
+                out=yt_bf[:, n // 2 % YT_BUFS, cols(PASS, n % 2)].rearrange("p (s t) -> p s t", t=PACK),
+                in_=bank[bk][:].rearrange("p (t s) -> p s t", t=PACK),
+            )
 
-        def y_quantize2(k):
-            sl = slice(W * k, W * (k + 1))
-            quantize(y_codes[:, sl], y_scale[:, sl], flat(yt_bf[:, 2 * (k % 2) : 2 * (k % 2) + 2, :]))
-
-        def words_store(lo, hi):
-            sl = slice(256 * lo, 256 * hi)
+        def y_planes(first, count):
+            sl = slice(PAIR * first, PAIR * (first + count))
+            at = first % YT_BUFS
+            quantize(y_codes[:, sl], y_scale[:, sl], flat(yt_bf[:, at : at + count, :]))
             nc.sync.dma_start(
                 out=out_1[0].rearrange("p m t -> p (m t)").bitcast(I32)[:, sl], in_=y_codes[:, sl].bitcast(I32)
             )
 
-        def scales_store(lo, hi):
-            sl = slice(256 * lo, 256 * hi)
-            for quad in range(4):
-                (nc.sync if lo == 0 else nc.scalar).dma_start(
-                    out=out_2[0, 4 * quad : 4 * quad + 4, sl].bitcast(I32),
-                    in_=y_scale[32 * quad : 32 * quad + 4, sl].bitcast(I32),
+        def scales_store(bi):
+            for quad in range(PACK):
+                nc.sync.dma_start(
+                    out=out_2[0, cols(4, quad), cols(S, bi)].bitcast(I32),
+                    in_=y_scale[32 * quad : 32 * quad + 4, cols(S, bi)].bitcast(I32),
                 )
 
-        def y_out(pair, h, bk, eng="A"):
-            y_evict(pair, h, bk, eng)
-            y_store_h(pair, h)
-
-        def planes2(k):
-            y_quantize2(k)
-            words_store(2 * k, 2 * k + 2)
-
-        def planes1(pair):
-            y_quantize(pair)
-            words_store(pair, pair + 1)
-
-        def setup():
-            nc.vector.memset(warm_in[:], 1.0)
-            nc.vector.memset(flat(psc_raw[:]).bitcast(I32), 0)
-            nc.vector.memset(csc[:].bitcast(I32), 0)
-            nc.scalar.activation(out=warm_out[:], in_=warm_in[:], func=ACT.Abs_reciprocal_sqrt)
-            make_identity(nc, ident_bf[:])
-            make_identity(nc, ident_f32[:])
-
         setup()
-        load_col('om')
+        load_col(om_col, om)
         load_p_words()
-        spread_om()
-        load_col('nu')
-        load_x(1)
+        load_col(nu_col, nu)
         load_x(0)
-        lor_sq4()
-        lor_ars(1)
+        load_col(b_col, b)
+        load_x(1)
         load_p_scales()
-        permute_p_words()
-        load_col('b')
         load_q(0)
-        x_interleave(1, 'V')
-        load_x(2)
-        x_interleave(0, 'V')
-        lor_ars(0)
-        lor_sq2(1)
-        permute_p_scales()
-        q_transpose(0, 0, 3)
-        x_quantize2(0)
-        q_transpose(0, 1, 6)
-        u_matmul(0, 1, 0)
-        q_evict(0, 0, 3, 'A')
         load_c()
-        u_matmul(0, 3, 7)
-        lor_sq2(0)
-        de_times_b()
-        u_matmul(0, 2, 5)
-        load_q(3)
-        g_imag(1)
-        u_evict(0, 3, 7, 'A')
+        load_x(2)
         load_q(1)
-        u_matmul(0, 0, 3)
-        q_evict(0, 1, 6, 'A')
-        q_transpose(1, 1, 4)
-        g_imag(0)
-        u_evict(0, 0, 3, 'A')
-        u_evict(0, 1, 0, 'A')
-        g_real(0)
-        g_quantize(1)
-        q_transpose(3, 0, 3)
-        k_matmul(1, 1, 0)
-        k_matmul(1, 3, 1)
-        k_matmul(1, 0, 2)
-        g_real(1)
         load_x(3)
-        f_mul(0, 1, 1, 0)
-        g_quantize(0)
-        u_evict(0, 2, 5, 'A')
-        q_transpose(3, 1, 0)
-        x_interleave(2, 'A')
-        f_mul(0, 1, 0, 2)
-        f_mul(0, 1, 3, 1)
-        k_matmul(0, 0, 5)
-        x_interleave(3, 'A')
-        k_matmul(0, 0, 7)
-        q_evict(3, 0, 3, 'A')
-        k_matmul(0, 2, 6)
         load_q(2)
-        k_matmul(0, 1, 2)
-        q_transpose(2, 0, 1)
-        q_evict(3, 1, 0, 'A')
-        f_mul(0, 0, 0, 7)
-        f_mul(0, 0, 1, 2)
-        f_mul(0, 0, 2, 6)
-        q_transpose(2, 1, 7)
-        q_transpose(1, 0, 2)
-        q_evict(2, 1, 7, 'A')
-        k_matmul(0, 3, 3)
-        q_evict(2, 0, 1, 'A')
-        q_evict(1, 0, 2, 'A')
-        k_matmul(1, 2, 6)
-        k_matmul(0, 3, 0)
-        x_quantize2(1)
-        f_mul(0, 0, 3, 3)
-        f_mul(0, 1, 2, 6)
-        u_matmul(1, 1, 7)
-        u_evict(1, 1, 7, 'A')
-        q_quantize2(1)
-        q_evict(1, 1, 4, 'A')
-        u_matmul(1, 2, 1)
-        u_matmul(1, 0, 2)
-        f_quantize2(0)
-        u_evict(1, 0, 2, 'A')
-        q_quantize2(0)
-        u_matmul(1, 3, 7)
-        f_mul(1, 0, 0, 5)
-        k_matmul(1, 2, 6)
-        u_evict(1, 3, 7, 'A')
-        k_matmul(0, 2, 2)
-        y_matmul(3, 1, 4)
-        u_evict(1, 2, 1, 'A')
-        y_out(3, 1, 4, 'A')
-        y_matmul(2, 0, 7)
-        y_out(2, 0, 7, 'A')
-        y_matmul(0, 0, 3)
-        y_cast(0, 0, 3)
-        y_matmul(0, 1, 4)
-        y_cast(0, 1, 4)
-        k_matmul(0, 1, 1)
-        y_out(0, 1, 4, 'A')
-        f_mul(1, 0, 3, 0)
-        f_mul(1, 1, 2, 6)
-        y_matmul(1, 1, 5)
-        f_mul(1, 0, 2, 2)
-        y_out(0, 0, 3, 'A')
-        k_matmul(1, 3, 7)
-        k_matmul(1, 0, 0)
-        f_mul(1, 0, 1, 1)
-        k_matmul(1, 1, 6)
-        f_mul(1, 1, 0, 0)
-        y_out(1, 1, 5, 'A')
-        y_matmul(2, 1, 1)
-        y_matmul(1, 0, 2)
-        f_quantize(1, 0)
-        y_out(2, 1, 1, 'A')
-        y_matmul(3, 0, 3)
-        y_pass(5, 0, 0, 0)
-        y_cast(1, 1, 5)
-        f_mul(1, 1, 1, 6)
-        y_out(3, 0, 3, 'A')
-        y_pass(6, 0, 1, 0)
-        f_mul(1, 1, 3, 7)
-        f_quantize(1, 1)
-        y_pass(7, 0, 4, 0)
-        y_pass(4, 0, 6, 0)
-        y_round2(1)
-        y_pass(5, 1, 5, 0)
-        y_pass(4, 1, 3, 0)
-        y_out(1, 0, 2, 'A')
-        y_pass(5, 1, 5, 1)
-        y_pass(5, 0, 0, 1)
-        y_cast(1, 0, 2)
-        y_pass(6, 0, 1, 1)
-        y_pass(4, 1, 3, 1)
-        y_pass(4, 0, 6, 1)
-        y_out(5, 1, 5, 'A')
-        y_out(5, 0, 0, 'V')
-        y_pass(6, 1, 2, 0)
-        y_out(6, 0, 1, 'A')
-        y_out(4, 1, 3, 'V')
-        y_pass(6, 1, 2, 1)
-        y_pass(7, 0, 4, 1)
-        y_out(4, 0, 6, 'A')
-        y_out(7, 0, 4, 'V')
-        y_transpose(0, 7)
-        y_transpose(1, 5)
-        y_transpose(3, 3)
-        y_out(6, 1, 2, 'A')
-        y_pass(7, 1, 0, 0)
-        yt_evict(0, 7, 'A')
-        y_pass(7, 1, 0, 1)
-        y_round2(2)
-        y_transpose(2, 1)
-        yt_evict(1, 5, 'A')
-        y_transpose(4, 7)
-        yt_evict(3, 3, 'A')
-        planes2(0)
-        y_round(6, 'V')
-        yt_evict(2, 1, 'A')
-        y_out(7, 1, 0, 'A')
-        y_transpose(5, 2)
-        planes2(1)
-        yt_evict(4, 7, 'A')
-        yt_matmul(7, 1, 3)
-        yt_evict(5, 2, 'V')
-        y_transpose(6, 6)
-        yt_round(7, 1, 3, 'A')
-        scales_store(0, 4)
-        yt_evict(6, 6, 'A')
-        planes2(2)
-        yt_matmul(7, 0, 5)
-        yt_round(7, 0, 5, 'A')
-        planes1(6)
-        planes1(7)
-        scales_store(4, 8)
+        load_q(3)
+
+        spread_om(0)
+        permute_p_words()
+        x_interleave(0, "vector")
+        x_interleave(1, "vector")
+        permute_p_scales()
+        x_quantize(0)
+        make_factors()
+        make_lorentz()
+        q_transpose(0, 0, 1)
+        q_transpose(0, 1, 2)
+        for j in range(PACK):
+            u_matmul(0, j, 4 + j)
+        q_transpose(1, 0, 3)
+        q_transpose(1, 1, 0)
+        q_evict(0, 0, 1)
+        q_evict(0, 1, 2)
+        for j in range(PACK):
+            u_evict(0, j, 4 + j)
+        x_interleave(2, "scalar")
+        x_interleave(3, "scalar")
+        q_evict(1, 0, 3)
+        q_evict(1, 1, 0)
+        g_product(0, 0)
+        g_product(0, 1)
+        g_product(1, 0)
+        g_quantize(0)
+        g_product(1, 1)
+
+        for j in range(PACK):
+            k_matmul(0, j, 4 + j)
+        f_product(0, 0, 0, 4)
+        g_quantize(1)
+        k_matmul(1, 0, 1)
+        k_matmul(1, 1, 2)
+        f_product(0, 0, 1, 5)
+        k_matmul(1, 2, 4)
+        k_matmul(1, 3, 5)
+        f_product(0, 0, 2, 6)
+        f_product(0, 0, 3, 7)
+        for a in range(2):
+            q_transpose(2, a, 6 + a)
+        for a in range(2):
+            q_evict(2, a, 6 + a)
+        f_product(0, 1, 0, 1)
+        f_product(0, 1, 1, 2)
+        for a in range(2):
+            q_transpose(3, a, 1 + a)
+        for a in range(2):
+            q_evict(3, a, 1 + a)
+        x_quantize(1)
+        f_product(0, 1, 2, 4)
+        f_product(0, 1, 3, 5)
+
+        y_banks = [6, 7, 4, 5]
+        k_banks = [3, 0, 1, 2]
+        k_matmul(0, 0, k_banks[0])
+        k_matmul(0, 1, k_banks[1])
+        for j in range(PACK):
+            u_matmul(1, j, y_banks[j])
+            u_evict(1, j, y_banks[j])
+        k_matmul(0, 2, k_banks[2])
+        k_matmul(0, 3, k_banks[3])
+        f_quantize(0, 0, 2)
+        q_quantize(0)
+
+        for n in range(8):
+            y_tile(n, y_banks[n % 4], "scalar")
+            if n < 4:
+                y_round_from_bank(n, y_banks[n % 4])
+            if 1 <= n <= PACK:
+                k_matmul(1, n - 1, k_banks[n - 1])
+            f_product(1, n // PACK, n % PACK, k_banks[n % PACK])
+            if n == 1:
+                q_quantize(1)
+            if n == 6:
+                y_transpose(0, k_banks[0])
+                y_transpose(1, k_banks[1])
+        f_quantize(1, 0, 1)
+        f_quantize(1, 1, 1)
+
+        yt_evict(0, k_banks[0], "vector")
+        yt_evict(1, k_banks[1], "vector")
+        y_round_two_pairs(2)
+        ring = k_banks[2:] + y_banks
+        for n in range(6):
+            y_tile(8 + n, ring[n], "scalar")
+            if n == 2:
+                y_planes(0, 2)
+        y_round_two_pairs(4)
+        for a in range(2):
+            y_transpose(2 + a, k_banks[a])
+        for a in range(2):
+            yt_evict(2 + a, k_banks[a], "scalar")
+        y_round_pair(6)
+        y_tile(14, ring[0], "vector")
+        y_planes(2, 2)
+        scales_store(0)
+        for pair in (4, 5, 6):
+            y_transpose(pair, ring[pair - 3])
+            yt_evict(pair, ring[pair - 3], "scalar")
+        y_planes(4, 2)
+        y_planes(6, 1)
+        yt_tile(15, ring[4])
+        y_tile(15, ring[5], "vector")
+        yt_tile(14, k_banks[0])
+        y_planes(7, 1)
+        scales_store(1)

from contextlib import ExitStack

import concourse.mybir as mybir
from concourse.masks import make_identity

B, S, D, M, N = 2, 1024, 512, 512, 512
FLOPS = 2 * (2 * M * N * D + B * M * S * D + 2 * B * S * M * D)

F32 = mybir.dt.float32
BF16 = mybir.dt.bfloat16
I32 = mybir.dt.int32
U32 = mybir.dt.uint32
U8 = mybir.dt.uint8
FP8X4 = mybir.dt.float8_e4m3fn_x4
FP4X4 = mybir.dt.float4_e2m1fn_x4
ALU = mybir.AluOpType
ACT = mybir.ActivationFunctionType

P = 128
PACK = 4
PASS = P * PACK
PAIR = 2 * P
RUN = 4
YT_BUFS = 4


def tile_cauchytransferfunctionfilter_x2_kernel(
    tc, x, p_words, p_scales, om, nu, b, c_words, c_scales, q, out_0, out_1, out_2
):
    nc = tc.nc
    with ExitStack() as ctx:
        sb = ctx.enter_context(tc.tile_pool(name="sb", bufs=1))
        ps = ctx.enter_context(tc.psum_pool(name="ps", bufs=1))
        ctx.enter_context(tc.manual_schedule())

        def tile(name, shape, dtype):
            return sb.tile(shape, dtype, name=name, align_bytes=64)

        def tiles(name, count, shape, dtype):
            return [tile("%s%d" % (name, i), shape, dtype) for i in range(count)]

        bank = [ps.tile([P, PASS], F32, name="bank%d" % i) for i in range(8)]

        ident_bf = tile("ident_bf", [P, P], BF16)
        ident_f32 = tile("ident_f32", [P, P], F32)
        table_in = tile("table_in", [P, 1], F32)
        table_out = tile("table_out", [P, 1], F32)
        om_col = tile("om_col", [P, PACK], BF16)
        nu_col = tile("nu_col", [P, PACK], BF16)
        b_col = tile("b_col", [P, PACK], BF16)
        om_row = tile("om_row", [P, M], BF16)
        lorentz = tile("lorentz", [P, PACK, M], F32)
        half_b = tile("half_b", [P, PACK], F32)
        de_b = tile("de_b", [P, PACK, M], F32)
        g_bf = tiles("g_bf", 2, [P, M, PACK], BF16)
        g_codes = tiles("g_codes", 2, [P, M], U32)
        g_scale = tiles("g_scale", 2, [P, M], U8)
        pw_raw = tile("pw_raw", [P, 2, 2 * M], U8)
        psc_raw = tile("psc_raw", [P, 2, M], U8)
        pw = tile("pw", [P, PACK, 2, 2 * P], U8)
        psc = tile("psc", [P, PACK, 2, P], U8)
        cw = tile("cw", [P, 2 * D], U8)
        csc = tile("csc", [P, D], U8)
        x_raw = tile("x_raw", [P, 4, PACK * D], BF16)
        x_bf = tile("x_bf", [P, 2, PACK * D], BF16)
        x_codes = tile("x_codes", [P, 4, D], U32)
        x_scale = tile("x_scale", [P, 4, D], U8)
        q_raw = tiles("q_raw", 4, [P, 2, 2 * M], BF16)
        q_bf = tile("q_bf", [P, 4, 2, 2 * PASS], BF16)
        q_codes = tile("q_codes", [P, 4, PASS], U32)
        q_scale = tile("q_scale", [P, 4, PASS], U8)
        u_sb = tiles("u_sb", 2, [P, PACK, PASS], F32)
        f_bf = tile("f_bf", [P, 2, PACK * D], BF16)
        f_codes = tile("f_codes", [P, 4, D], U32)
        f_scale = tile("f_scale", [P, 4, D], U8)
        y32 = tile("y32", [P, 8, 2, D], F32)
        y_bf = tile("y_bf", [P, 4, 2 * D], BF16)
        yt_bf = tile("yt_bf", [P, YT_BUFS, 2 * D], BF16)
        y_codes = tile("y_codes", [P, B * S], U32)
        y_scale = tile("y_scale", [P, B * S], U8)

        x_grouped = [x_bf[:], x_raw[:, 0:2, :]]
        y_rounded = [q_bf[:, 0], q_bf[:, 1], y_bf[:, 0:2, :], y_bf[:, 2:4, :]]
        y_words = {}

        def copy_on(engine, dst, src):
            if engine == "vector":
                nc.vector.tensor_copy(out=dst, in_=src)
            else:
                nc.scalar.copy(out=dst, in_=src)

        def flat(ap):
            return ap.rearrange("p a b -> p (a b)")

        def cols(width, i):
            return slice(width * i, width * (i + 1))

        def quantize(codes, scale, src):
            nc.vector.quantize_mx(out=codes.bitcast(FP8X4), scales=scale, in_=src)

        def setup():
            nc.vector.memset(table_in[:], 1.0)
            nc.vector.memset(flat(psc_raw[:]).bitcast(I32), 0)
            nc.vector.memset(csc[:].bitcast(I32), 0)
            nc.scalar.activation(out=table_out[:], in_=table_in[:], func=ACT.Abs_reciprocal_sqrt)
            make_identity(nc, ident_bf[:])
            make_identity(nc, ident_f32[:])

        def load_col(dst, vec):
            nc.sync.dma_start(out=dst[:], in_=vec.rearrange("(p t) -> p t", t=PACK))

        def load_x(i):
            bi, g = divmod(i, 2)
            nc.sync.dma_start(
                out=x_raw[:, i, :], in_=x[bi, cols(PASS, g), :].rearrange("(p t) d -> p (t d)", t=PACK)
            )

        def load_q(i):
            half, part = divmod(i, 2)
            nc.sync.dma_start(
                out=q_raw[i][:],
                in_=q[part, cols(PASS, half), :].rearrange("(a p h) m -> p a (h m)", a=2, h=2),
            )

        def load_p_words():
            nc.sync.dma_start(out=pw_raw[:].bitcast(I32), in_=p_words.rearrange("g p n -> p g n").bitcast(I32))

        def load_p_scales():
            for quad in range(PACK):
                nc.sync.dma_start(
                    out=psc_raw[32 * quad : 32 * quad + 4, :, :].bitcast(I32),
                    in_=p_scales[:, cols(4, quad), :].rearrange("g r n -> r g n").bitcast(I32),
                )

        def load_c():
            nc.sync.dma_start(out=cw[:].bitcast(I32), in_=c_words[0].bitcast(I32))
            for quad in range(PACK):
                nc.sync.dma_start(
                    out=csc[32 * quad : 32 * quad + 4, :].bitcast(I32),
                    in_=c_scales[0, cols(4, quad), :].bitcast(I32),
                )

        def permute_p_words():
            nc.vector.tensor_copy(
                out=pw[:].rearrange("p t g (w e) -> p t (g w) e", e=2),
                in_=pw_raw[:].rearrange("p g (w t e) -> p t (g w) e", t=PACK, e=2),
            )

        def permute_p_scales():
            nc.vector.tensor_copy(
                out=psc[:].rearrange("p t g w -> p t (g w)"),
                in_=psc_raw[:].rearrange("p g (w t) -> p t (g w)", t=PACK),
            )

        def x_interleave(i, engine):
            copy_on(
                engine,
                x_grouped[i // 2][:, i % 2, :].rearrange("p (c r t) -> p c t r", r=RUN, t=PACK),
                x_raw[:, i, :].rearrange("p (t c r) -> p c t r", r=RUN, t=PACK),
            )

        def x_quantize(bi):
            sl = cols(2, bi)
            quantize(flat(x_codes[:, sl, :]), flat(x_scale[:, sl, :]), flat(x_grouped[bi]))

        def spread_om(bk):
            view = bank[bk][:].bitcast(BF16)
            for t in range(PACK):
                nc.tensor.transpose(view[:, cols(P, t)], om_col[:, t : t + 1].to_broadcast([P, P]), ident_bf[:])
            nc.scalar.copy(out=om_row[:], in_=view[:, 0:M])

        def make_lorentz():
            for t in range(PACK):
                nc.scalar.activation(
                    out=lorentz[:, t, :], in_=om_row[:], func=ACT.Square, bias=nu_col[:, t : t + 1], scale=-1.0
                )
            halves = [lorentz[:, :, cols(M // 2, half)] for half in range(2)]
            for ap in halves:
                nc.scalar.activation(out=ap, in_=ap, func=ACT.Abs_reciprocal_sqrt, bias=0.25)
            for ap in halves:
                nc.scalar.activation(out=ap, in_=ap, func=ACT.Square)

        def make_factors():
            nc.gpsimd.tensor_scalar(
                out=half_b[:], in0=b_col[:], scalar1=0.5, scalar2=1.0, op0=ALU.mult, op1=ALU.mult
            )
            for t in range(PACK):
                nc.vector.tensor_scalar(
                    out=de_b[:, t, :], in0=om_row[:], scalar1=nu_col[:, t : t + 1], scalar2=b_col[:, t : t + 1],
                    op0=ALU.subtract, op1=ALU.mult,
                )

        def g_product(part, half):
            sl = cols(M // 2, half)
            if part == 0:
                factor = half_b[:].unsqueeze(1).unsqueeze(3).to_broadcast([P, M // 2 // RUN, PACK, RUN])
            else:
                factor = de_b[:, :, sl].rearrange("p t (c r) -> p c t r", r=RUN)
            nc.vector.tensor_tensor(
                out=g_bf[part][:, sl, :].rearrange("p (c r) t -> p c t r", r=RUN),
                in0=lorentz[:, :, sl].rearrange("p t (c r) -> p c t r", r=RUN), in1=factor, op=ALU.mult,
            )

        def g_quantize(part):
            quantize(g_codes[part][:], g_scale[part][:], flat(g_bf[part][:]))

        def q_transpose(i, a, bk):
            words = q_raw[i][:, a, :].bitcast(F32)
            for h in range(2):
                for u in range(2):
                    nc.tensor.transpose(
                        bank[bk][:, cols(P, 2 * h + u)], words[:, PAIR * h + u : PAIR * (h + 1) : 2], ident_f32[:]
                    )

        def q_evict(i, a, bk):
            nc.scalar.copy(
                out=q_bf[:, i, a, :].bitcast(F32).rearrange("p (s r) -> p s r", r=4),
                in_=bank[bk][:].rearrange("p (r s) -> p s r", r=4),
            )

        def q_quantize(half):
            sl = cols(2, half)
            quantize(
                flat(q_codes[:, sl, :]), flat(q_scale[:, sl, :]), q_bf[:, sl].rearrange("p c a w -> p (c a w)")
            )

        def u_matmul(bi, j, bk):
            for t in range(PACK):
                for g in range(2):
                    nc.tensor.matmul_mx(
                        out=bank[bk][:, cols(P, t)],
                        lhsT=pw[:, t, g, :].bitcast(FP4X4), lhsT_scale=psc[:, t, g, :],
                        rhs=x_codes[:, 2 * bi + g, cols(P, j)].bitcast(FP8X4),
                        rhs_scale=x_scale[:, 2 * bi + g, cols(P, j)],
                        start=(g == 0), stop=(g == 1),
                    )

        def k_matmul(part, j, bk):
            for t in range(PACK):
                nc.tensor.matmul_mx(
                    out=bank[bk][:, cols(P, t)],
                    lhsT=g_codes[part][:, cols(P, t)].bitcast(FP8X4), lhsT_scale=g_scale[part][:, cols(P, t)],
                    rhs=cw[:, cols(2 * P, j)].bitcast(FP4X4), rhs_scale=csc[:, cols(P, j)],
                    start=True, stop=True,
                )

        def in_f_order(bk):
            return bank[bk][:].rearrange("p (t a e) -> p e a t", t=PACK, e=PACK)

        def u_chunk(bi, j):
            return u_sb[bi][:, j, :].rearrange("p (e a t) -> p e a t", e=PACK, t=PACK)

        def u_evict(bi, j, bk):
            nc.scalar.copy(out=u_chunk(bi, j), in_=in_f_order(bk))

        def f_product(bi, part, j, bk):
            nc.vector.tensor_tensor(
                out=f_bf[:, part, :].rearrange("p (e w t) -> p e w t", e=PACK, t=PACK)[:, :, cols(P // PACK, j), :],
                in0=in_f_order(bk), in1=u_chunk(bi, j), op=ALU.mult,
            )

        def f_quantize(bi, first, count):
            sl = slice(2 * bi + first, 2 * bi + first + count)
            quantize(flat(f_codes[:, sl, :]), flat(f_scale[:, sl, :]), flat(f_bf[:, first : first + count, :]))

        def tile_operands(n, part):
            bi, rows = divmod(n, S // P)
            half, place = divmod(rows, PASS // P)
            i = 2 * half + part
            return q_codes[:, i, cols(P, place)].bitcast(FP8X4), q_scale[:, i, cols(P, place)], 2 * bi + part

        def y_tile(n, bk, engine):
            for part in range(2):
                codes, scale, fi = tile_operands(n, part)
                nc.tensor.matmul_mx(
                    out=bank[bk][:], lhsT=codes, lhsT_scale=scale,
                    rhs=f_codes[:, fi, :].bitcast(FP8X4), rhs_scale=f_scale[:, fi, :],
                    start=(part == 0), stop=(part == 1),
                )
            dst = y32[:, n // 2, n % 2, :]
            copy_on(
                engine, dst.rearrange("p (w e) -> p w e", e=PACK), bank[bk][:].rearrange("p (e w) -> p w e", e=PACK)
            )
            bi, rows = divmod(n, S // P)
            nc.sync.dma_start(out=out_0[bi, cols(P, rows), :], in_=dst)

        def as_words(ap):
            return ap.bitcast(F32).rearrange("p (u w) -> p u w", u=2)

        def y_round_from_bank(n, bk):
            pair, h = divmod(n, 2)
            dst = y_rounded[pair // 2][:, pair % 2, :]
            nc.scalar.copy(
                out=dst.rearrange("p (u h w e) -> p h u w e", u=2, h=2, e=2)[:, h],
                in_=bank[bk][:].rearrange("p (u e w) -> p u w e", u=2, e=2),
            )
            y_words[pair] = as_words(dst)

        def y_round_pair(pair):
            dst = y_rounded[pair // 2][:, pair % 2, :]
            nc.vector.tensor_copy(
                out=dst.rearrange("p (u w e) -> p u w e", u=2, e=2),
                in_=flat(y32[:, pair]).rearrange("p (w u e) -> p u w e", u=2, e=2),
            )
            y_words[pair] = as_words(dst)

        def y_round_two_pairs(first):
            dst = flat(y_rounded[first // 2])
            nc.vector.tensor_copy(
                out=dst.rearrange("p (u w e) -> p u w e", u=2, e=2),
                in_=y32[:, first : first + 2].rearrange("p a h (w u e) -> p u (a h w) e", u=2, e=2),
            )
            for a in range(2):
                y_words[first + a] = as_words(dst)[:, :, cols(PAIR, a)]

        def y_transpose(pair, bk):
            for u in range(2):
                for h in range(2):
                    nc.tensor.transpose(
                        bank[bk][:, cols(P, 2 * u + h)], y_words[pair][:, u, cols(P, h)], ident_f32[:]
                    )

        def yt_evict(pair, bk, engine):
            copy_on(
                engine,
                yt_bf[:, pair % YT_BUFS, :].bitcast(F32).rearrange("p (s u) -> p s u", u=2),
                bank[bk][:].rearrange("p (u s) -> p s u", u=2),
            )

        def yt_tile(n, bk):
            for t in range(PACK):
                for part in range(2):
                    codes, scale, fi = tile_operands(n, part)
                    nc.tensor.matmul_mx(
                        out=bank[bk][:, cols(P, t)],
                        lhsT=f_codes[:, fi, cols(P, t)].bitcast(FP8X4), lhsT_scale=f_scale[:, fi, cols(P, t)],
                        rhs=codes, rhs_scale=scale, start=(part == 0), stop=(part == 1),
                    )
            nc.scalar.copy(
                out=yt_bf[:, n // 2 % YT_BUFS, cols(PASS, n % 2)].rearrange("p (s t) -> p s t", t=PACK),
                in_=bank[bk][:].rearrange("p (t s) -> p s t", t=PACK),
            )

        def y_planes(first, count):
            sl = slice(PAIR * first, PAIR * (first + count))
            at = first % YT_BUFS
            quantize(y_codes[:, sl], y_scale[:, sl], flat(yt_bf[:, at : at + count, :]))
            nc.sync.dma_start(
                out=out_1[0].rearrange("p m t -> p (m t)").bitcast(I32)[:, sl], in_=y_codes[:, sl].bitcast(I32)
            )

        def scales_store(bi):
            for quad in range(PACK):
                nc.sync.dma_start(
                    out=out_2[0, cols(4, quad), cols(S, bi)].bitcast(I32),
                    in_=y_scale[32 * quad : 32 * quad + 4, cols(S, bi)].bitcast(I32),
                )

        setup()
        load_col(om_col, om)
        load_p_words()
        load_col(nu_col, nu)
        load_x(0)
        load_col(b_col, b)
        load_x(1)
        load_p_scales()
        load_q(0)
        load_c()
        load_x(2)
        load_q(1)
        load_x(3)
        load_q(2)
        load_q(3)

        spread_om(0)
        permute_p_words()
        x_interleave(0, "vector")
        x_interleave(1, "vector")
        permute_p_scales()
        x_quantize(0)
        make_factors()
        make_lorentz()
        q_transpose(0, 0, 1)
        q_transpose(0, 1, 2)
        for j in range(PACK):
            u_matmul(0, j, 4 + j)
        q_transpose(1, 0, 3)
        q_transpose(1, 1, 0)
        q_evict(0, 0, 1)
        q_evict(0, 1, 2)
        for j in range(PACK):
            u_evict(0, j, 4 + j)
        x_interleave(2, "scalar")
        x_interleave(3, "scalar")
        q_evict(1, 0, 3)
        q_evict(1, 1, 0)
        g_product(0, 0)
        g_product(0, 1)
        g_product(1, 0)
        g_quantize(0)
        g_product(1, 1)

        for j in range(PACK):
            k_matmul(0, j, 4 + j)
        f_product(0, 0, 0, 4)
        g_quantize(1)
        k_matmul(1, 0, 1)
        k_matmul(1, 1, 2)
        f_product(0, 0, 1, 5)
        k_matmul(1, 2, 4)
        k_matmul(1, 3, 5)
        f_product(0, 0, 2, 6)
        f_product(0, 0, 3, 7)
        for a in range(2):
            q_transpose(2, a, 6 + a)
        for a in range(2):
            q_evict(2, a, 6 + a)
        f_product(0, 1, 0, 1)
        f_product(0, 1, 1, 2)
        for a in range(2):
            q_transpose(3, a, 1 + a)
        for a in range(2):
            q_evict(3, a, 1 + a)
        x_quantize(1)
        f_product(0, 1, 2, 4)
        f_product(0, 1, 3, 5)

        y_banks = [6, 7, 4, 5]
        k_banks = [3, 0, 1, 2]
        k_matmul(0, 0, k_banks[0])
        k_matmul(0, 1, k_banks[1])
        for j in range(PACK):
            u_matmul(1, j, y_banks[j])
            u_evict(1, j, y_banks[j])
        k_matmul(0, 2, k_banks[2])
        k_matmul(0, 3, k_banks[3])
        f_quantize(0, 0, 2)
        q_quantize(0)

        for n in range(8):
            y_tile(n, y_banks[n % 4], "scalar")
            if n < 4:
                y_round_from_bank(n, y_banks[n % 4])
            if 1 <= n <= PACK:
                k_matmul(1, n - 1, k_banks[n - 1])
            f_product(1, n // PACK, n % PACK, k_banks[n % PACK])
            if n == 1:
                q_quantize(1)
            if n == 6:
                y_transpose(0, k_banks[0])
                y_transpose(1, k_banks[1])
        f_quantize(1, 0, 1)
        f_quantize(1, 1, 1)

        yt_evict(0, k_banks[0], "vector")
        yt_evict(1, k_banks[1], "vector")
        y_round_two_pairs(2)
        ring = k_banks[2:] + y_banks
        for n in range(6):
            y_tile(8 + n, ring[n], "scalar")
            if n == 2:
                y_planes(0, 2)
        y_round_two_pairs(4)
        for a in range(2):
            y_transpose(2 + a, k_banks[a])
        for a in range(2):
            yt_evict(2 + a, k_banks[a], "scalar")
        y_round_pair(6)
        y_tile(14, ring[0], "vector")
        y_planes(2, 2)
        scales_store(0)
        for pair in (4, 5, 6):
            y_transpose(pair, ring[pair - 3])
            yt_evict(pair, ring[pair - 3], "scalar")
        y_planes(4, 2)
        y_planes(6, 1)
        yt_tile(15, ring[4])
        y_tile(15, ring[5], "vector")
        yt_tile(14, k_banks[0])
        y_planes(7, 1)
        scales_store(1)
